import numpy as np
import ml_dtypes


def mxq(x, axis, fmt="e4m3"):
    dtype, down = {"e4m3": (ml_dtypes.float8_e4m3fn, 7), "e5m2": (ml_dtypes.float8_e5m2, 14)}[fmt]
    v = np.moveaxis(np.asarray(x, np.float32).astype(ml_dtypes.bfloat16).astype(np.float64), axis, -1)
    blocks = v.reshape(v.shape[:-1] + (-1, 32))
    amax = np.abs(blocks).max(-1, keepdims=True)
    byte = np.maximum(np.where(amax > 0, np.frexp(amax)[1] - 1 + 127, 0) - down, 1)
    scale = np.exp2(byte - 127.0)
    codes = (blocks / scale).astype(np.float32).astype(dtype).astype(np.float64)
    return np.moveaxis((codes * scale).reshape(v.shape), -1, axis)


WIDE = False


def mx_kscale(k):
    if not WIDE:
        return np.ones(k)
    levels = np.array([10, -10, 5, -5, 0])
    if k % 512:
        return np.exp2(np.random.permutation(np.resize(levels, k // 32))).repeat(32)
    a = np.empty((k // 512, 16))
    for p in range(k // 512):
        a[p, :8] = np.random.permutation(np.resize(levels, 8))
        for g in range(8):
            far = levels[np.abs(levels - a[p, g]) >= 10]
            a[p, g + 8] = far[np.random.randint(len(far))]
    return np.exp2(a.ravel()).repeat(32)


def f64(x):
    return np.asarray(x).astype(np.float64)


def striped(idx):
    return np.tile(np.asarray(idx).reshape(-1, 16).T, (8, 1)).astype(np.uint16)


def unstriped(offs):
    return offs[:16].T.reshape(-1).astype(np.int64)

def rot(x):
    y = x.reshape(x.shape[0], -1, 2, x.shape[2])
    return np.stack([-y[:, :, 1], y[:, :, 0]], axis=2).reshape(x.shape)


def bf(x):
    return np.asarray(x, np.float32).astype(ml_dtypes.bfloat16)


def planes(Y):
    r, m = Y.shape
    b = f64(bf(Y)).reshape(r // 32, 32, m)
    amax = np.abs(b).max(1)
    byte = np.clip(np.where(amax > 0, np.frexp(amax)[1] - 1 + 127 - 7, 1), 1, 254)
    codes = (b * np.exp2(127.0 - byte)[:, None, :]).reshape(r, m).astype(np.float32).astype(ml_dtypes.float8_e4m3fn).view(np.uint8)
    words = codes.reshape(r // 512, 128, 4, m).transpose(0, 1, 3, 2)
    return np.ascontiguousarray(words), np.ascontiguousarray(byte.astype(np.uint8).reshape(r // 512, 16, m))


B, N, T, D, NQ = 1, 512, 2048, 512, 256


def setup_inputs():
    n = np.random.standard_normal
    idx = np.random.permutation(T)[:B * N]
    idx2 = np.random.permutation(1024)[:B * N]
    s = mx_kscale(D)[:, None]
    return {
        "qT": (n((B, D, NQ)) * s * (1.00 / np.sqrt(D))).astype(np.float32),
        "kT": (np.clip(np.round(n((D, T)) * 16), -64, 64) / 16 / s).astype(np.float32),
        "cT": (np.repeat(np.round(np.cos(np.arange(D // 2)[:, None] * 0.11 + np.arange(1024)[None] * 0.37) * 64) / 64, 2, axis=0)).astype(np.float32),
        "wT": (np.repeat(np.round(np.sin(np.arange(D // 2)[:, None] * 0.11 + np.arange(1024)[None] * 0.37) * 64) / 64, 2, axis=0)).astype(np.float32),
        "ls": (np.random.uniform(7.8, 8.4, (B, 1, NQ))).astype(np.float32),
        "offs": striped(idx),
        "offs2": striped(idx2),
    }


def reference(qT, kT, cT, wT, ls, offs, offs2):
    idx = unstriped(offs)
    idx2 = unstriped(offs2)
    pick = lambda x, which: x[:, which].reshape(x.shape[0], B, -1).transpose(1, 0, 2)
    kg = pick(f64(kT), idx)
    cg = pick(f64(cT), idx2)
    wg = pick(f64(wT), idx2)
    ug = mxq(kg * cg + rot(kg) * wg, 1, "e4m3")
    qq = mxq(f64(qT), 1, "e4m3")
    a = ug.transpose(0, 2, 1) @ qq
    y = np.exp(a - f64(ls))
    Y = y[0]
    words, scales = planes(Y)
    return Y, words, scales

@@ -1,0 +1,137 @@
+from contextlib import ExitStack
+
+import concourse.mybir as mybir
+from concourse.masks import make_identity
+
+N, T, D, NQ, NPOS = 512, 2048, 512, 256, 1024
+FLOPS = 2 * N * D * NQ
+BYTES = 4 * (D * NQ + D * T + D * NPOS + NQ + N * NQ) + 2 * 128 * 32 * 2 + 128 * NQ * 4 + 16 * NQ
+
+F32 = mybir.dt.float32
+BF16 = mybir.dt.bfloat16
+I32 = mybir.dt.int32
+U32 = mybir.dt.uint32
+U16 = mybir.dt.uint16
+U8 = mybir.dt.uint8
+FP8X4 = mybir.dt.float8_e4m3fn_x4
+MULT = mybir.AluOpType.mult
+ADD = mybir.AluOpType.add
+EXP = mybir.ActivationFunctionType.Exp
+
+P = 128
+HALF = N // 2
+
+
+def tile_attend_plw_rope_f_topk_kernel(tc, qT, kT, cT, wT, ls, offs, offs2, out_0, out_1, out_2):
+    nc = tc.nc
+    with ExitStack() as ctx:
+        sb = ctx.enter_context(tc.tile_pool(name="sb", bufs=1))
+        ps = ctx.enter_context(tc.psum_pool(name="ps", bufs=1))
+
+        tok = sb.tile([P, N // 16], U16, name="tok")
+        pos = sb.tile([P, N // 16], U16, name="pos")
+        k_rows = kT.rearrange("(p t) n -> p t n", t=4)
+        c_rows = cT.rearrange("(p t) n -> p t n", t=4)
+        w_rows = wT.rearrange("(p t) n -> p t n", t=4)
+        k_win = [sb.tile([P, T], F32, name="k_win%d" % t) for t in range(4)]
+        c_win = [sb.tile([P, NPOS], F32, name="c_win%d" % j) for j in range(2)]
+        w_win = [sb.tile([P, NPOS], F32, name="w_win%d" % j) for j in range(2)]
+        q_raw = sb.tile([P, 4, NQ], F32, name="q_raw")
+        ls_col = sb.tile([P, 2], F32, name="ls_col")
+
+        nc.sync.dma_start(c_win[0][:], c_rows[:, 0, :])
+        nc.sync.dma_start(pos[:], offs2)
+        nc.sync.dma_start(w_win[0][:], w_rows[:, 0, :])
+        nc.sync.dma_start(tok[:], offs)
+        nc.sync.dma_start(k_win[0][:], k_rows[:, 0, :])
+        nc.sync.dma_start(k_win[1][:], k_rows[:, 1, :])
+        nc.sync.dma_start(c_win[1][:], c_rows[:, 2, :])
+        nc.sync.dma_start(w_win[1][:], w_rows[:, 2, :])
+        nc.sync.dma_start(k_win[2][:], k_rows[:, 2, :])
+        nc.sync.dma_start(k_win[3][:], k_rows[:, 3, :])
+        nc.sync.dma_start(q_raw[:], qT[0].rearrange("(p t) n -> p t n", t=4))
+        with nc.allow_non_contiguous_dma(reason="one log-sum-exp to a partition"):
+            nc.sync.dma_start(ls_col[:], ls[0, 0, :].rearrange("(h p) -> p h", p=P))
+
+        ident = sb.tile([P, P], F32, name="ident")
+        make_identity(nc, ident[:])
+        warm = sb.tile([P, 1], F32, name="warm")
+        nc.scalar.activation(warm[:], ident[:, 0:1], EXP)
+
+        prod_even = sb.tile([P, 4, N], F32, name="prod_even")
+        prod_odd = sb.tile([P, 4, N], F32, name="prod_odd")
+        trig = [sb.tile([P, 3, N], F32, name="trig%d" % j) for j in range(2)]
+        kg = [sb.tile([P, N], F32, name="kg%d" % t) for t in range(4)]
+
+        def product(dst, key, factors, cols):
+            width = cols.stop - cols.start
+            nc.vector.tensor_tensor(dst[:, :, cols], key[:, cols].unsqueeze(1).to_broadcast([P, 2, width]), factors[:, :, cols], MULT)
+
+        whole = slice(0, N)
+        halves = [slice(0, HALF), slice(HALF, N)]
+        for j in range(2):
+            nc.vector.tensor_copy(trig[j][:, 1, :], c_win[j][:].indirect(pos[:]))
+            nc.vector.tensor_copy(trig[j][:, 2, :], w_win[j][:].indirect(pos[:]))
+            nc.scalar.mul(trig[j][:, 0, :], trig[j][:, 2, :], -1.0)
+            pair = slice(2 * j, 2 * j + 2)
+            for t, dst, factors in ((2 * j, prod_even, trig[j][:, 1:3, :]), (2 * j + 1, prod_odd, trig[j][:, 0:2, :])):
+                for cols in halves:
+                    nc.vector.tensor_copy(kg[t][:, cols], k_win[t][:].indirect(tok[:, cols.start // 16 : cols.stop // 16]))
+                for cols in halves:
+                    product(dst[:, pair, :], kg[t], factors, cols)
+
+        q_bf = sb.tile([P, NQ * 4], BF16, name="q_bf", align_bytes=64)
+        q_codes = sb.tile([P, NQ], U32, name="q_codes", align_bytes=64)
+        q_scales = sb.tile([P, NQ], U8, name="q_scales", align_bytes=64)
+        nc.scalar.copy(q_bf[:].rearrange("p (c i t) -> p c t i", i=4, t=4), q_raw[:].rearrange("p t (c i) -> p c t i", i=4))
+        neg_ls = sb.tile([P, 2], F32, name="neg_ls")
+        nc.scalar.mul(neg_ls[:], ls_col[:], -1.0)
+
+        yT = [sb.tile([P, 4, P], F32, name="yT%d" % h) for h in range(2)]
+        for a in range(4):
+            cols = slice(a * P, (a + 1) * P)
+            u_bf = sb.tile([P, P * 4], BF16, name="u_bf%d" % a, align_bytes=64)
+            u_codes = sb.tile([P, P], U32, name="u_codes%d" % a, align_bytes=64)
+            u_scales = sb.tile([P, P], U8, name="u_scales%d" % a, align_bytes=64)
+            nc.vector.tensor_tensor(
+                u_bf[:].rearrange("p (c i t) -> p c t i", i=4, t=4),
+                prod_even[:, :, cols].rearrange("p t (c i) -> p c t i", i=4),
+                prod_odd[:, :, cols].rearrange("p t (c i) -> p c t i", i=4),
+                ADD,
+            )
+            if a == 0:
+                nc.vector.quantize_mx(out=q_codes[:].bitcast(FP8X4), scales=q_scales[:], in_=q_bf[:])
+            nc.vector.quantize_mx(out=u_codes[:].bitcast(FP8X4), scales=u_scales[:], in_=u_bf[:])
+            score = ps.tile([P, 2, P], F32, name="score%d" % a)
+            for h in range(2):
+                qs = slice(h * P, (h + 1) * P)
+                nc.tensor.matmul_mx(
+                    out=score[:, h, :], lhsT=q_codes[:, qs].bitcast(FP8X4), lhsT_scale=q_scales[:, qs],
+                    rhs=u_codes[:].bitcast(FP8X4), rhs_scale=u_scales[:], start=True, stop=True,
+                )
+            for h in range(2):
+                nc.scalar.activation(
+                    yT[h][:, :, a * 32 : (a + 1) * 32], score[:, h, :].rearrange("p (s r) -> p r s", r=4), EXP, bias=neg_ls[:, h : h + 1]
+                )
+
+        y = [sb.tile([P, 4, P], F32, name="y%d" % h) for h in range(2)]
+        y_bf = [sb.tile([P, P * 4], BF16, name="y_bf%d" % h, align_bytes=64) for h in range(2)]
+        y_codes = sb.tile([P, NQ], U32, name="y_codes", align_bytes=64)
+        y_scales = sb.tile([P, NQ], U8, name="y_scales", align_bytes=64)
+        out_rows = out_0.rearrange("(p r) q -> p r q", r=4)
+        turned = [ps.tile([P, 4, P], F32, name="turned%d" % h) for h in range(2)]
+        for h in range(2):
+            for r in range(4):
+                nc.tensor.transpose(turned[h][:, r, :], yT[h][:, r, :], ident[:])
+        for h in range(2):
+            qs = slice(h * P, (h + 1) * P)
+            nc.vector.tensor_copy(y_bf[h][:].rearrange("p (q r) -> p q r", r=4), turned[h][:].rearrange("p r q -> p q r"))
+            other = 1 - h
+            nc.scalar.copy(y[other][:], turned[other][:])
+            queue = nc.sync if h == 0 else nc.scalar
+            queue.dma_start(out_rows[:, :, other * P : (other + 1) * P], y[other][:])
+            nc.vector.quantize_mx(out=y_codes[:, qs].bitcast(FP8X4), scales=y_scales[:, qs], in_=y_bf[h][:])
+        nc.sync.dma_start(out_1[0].rearrange("p q x -> p (q x)").bitcast(I32), y_codes[:].bitcast(I32))
+        for quad in range(4):
+            queue = nc.scalar if quad % 2 == 0 else nc.sync
+            queue.dma_start(out_2[0, 4 * quad : 4 * quad + 4, :].bitcast(I32), y_scales[32 * quad : 32 * quad + 4, :].bitcast(I32))

@@ -36,7 +36,7 @@ def tile_attend_plw_rope_f_topk_kernel(tc, qT, kT, cT, wT, ls, offs, offs2, out_
         k_win = [sb.tile([P, T], F32, name="k_win%d" % t) for t in range(4)]
         c_win = [sb.tile([P, NPOS], F32, name="c_win%d" % j) for j in range(2)]
         w_win = [sb.tile([P, NPOS], F32, name="w_win%d" % j) for j in range(2)]
-        q_raw = sb.tile([P, 4, NQ], F32, name="q_raw")
+        q_raw = [sb.tile([P, 4, P], F32, name="q_raw%d" % h) for h in range(2)]
         ls_col = sb.tile([P, 2], F32, name="ls_col")
 
         nc.sync.dma_start(c_win[0][:], c_rows[:, 0, :])
@@ -49,7 +49,8 @@ def tile_attend_plw_rope_f_topk_kernel(tc, qT, kT, cT, wT, ls, offs, offs2, out_
         nc.sync.dma_start(w_win[1][:], w_rows[:, 2, :])
         nc.sync.dma_start(k_win[2][:], k_rows[:, 2, :])
         nc.sync.dma_start(k_win[3][:], k_rows[:, 3, :])
-        nc.sync.dma_start(q_raw[:], qT[0].rearrange("(p t) n -> p t n", t=4))
+        for h in range(2):
+            nc.sync.dma_start(q_raw[h][:], qT[0].rearrange("(p t) n -> p t n", t=4)[:, :, h * P : (h + 1) * P])
         with nc.allow_non_contiguous_dma(reason="one log-sum-exp to a partition"):
             nc.sync.dma_start(ls_col[:], ls[0, 0, :].rearrange("(h p) -> p h", p=P))
 
@@ -67,7 +68,7 @@ def tile_attend_plw_rope_f_topk_kernel(tc, qT, kT, cT, wT, ls, offs, offs2, out_
             width = cols.stop - cols.start
             nc.vector.tensor_tensor(dst[:, :, cols], key[:, cols].unsqueeze(1).to_broadcast([P, 2, width]), factors[:, :, cols], MULT)
 
-        whole = slice(0, N)
+        words = [sb.tile([P, 2, P], F32, name="words%d" % c) for c in range(4)]
         halves = [slice(0, HALF), slice(HALF, N)]
         for j in range(2):
             nc.vector.tensor_copy(trig[j][:, 1, :], c_win[j][:].indirect(pos[:]))
@@ -77,15 +78,32 @@ def tile_attend_plw_rope_f_topk_kernel(tc, qT, kT, cT, wT, ls, offs, offs2, out_
             for t, dst, factors in ((2 * j, prod_even, trig[j][:, 1:3, :]), (2 * j + 1, prod_odd, trig[j][:, 0:2, :])):
                 for cols in halves:
                     nc.vector.tensor_copy(kg[t][:, cols], k_win[t][:].indirect(tok[:, cols.start // 16 : cols.stop // 16]))
-                for cols in halves:
-                    product(dst[:, pair, :], kg[t], factors, cols)
+                if t < 3:
+                    for cols in halves:
+                        product(dst[:, pair, :], kg[t], factors, cols)
+            if j == 0:
+                back = ps.tile([P, 4, P], F32, name="back", tag="turned0")
+                for a in range(2):
+                    summed = ps.tile([P, 2, 2, P], F32, name="summed%d" % a, tag="late%d" % a)
+                    for b in range(2):
+                        cols = slice((2 * a + b) * P, (2 * a + b + 1) * P)
+                        for e in range(2):
+                            nc.tensor.matmul(summed[:, b, e, :], prod_even[:, e, cols], ident[:], start=True, stop=False, is_transpose=True)
+                            nc.tensor.matmul(summed[:, b, e, :], prod_odd[:, e, cols], ident[:], start=False, stop=True, is_transpose=True)
+                    rounded = sb.tile([P, 2, 2 * P], BF16, name="rounded%d" % a)
+                    nc.scalar.copy(rounded[:].rearrange("s b (p e) -> s b p e", e=2), summed[:].rearrange("s b e p -> s b p e"))
+                    for b in range(2):
+                        nc.tensor.transpose(back[:, 2 * a + b, :], rounded[:, b, :].bitcast(F32), ident[:])
+                for c in range(4):
+                    nc.scalar.copy(words[c][:, 0, :], back[:, c, :])
 
-        q_bf = sb.tile([P, NQ * 4], BF16, name="q_bf", align_bytes=64)
-        q_codes = sb.tile([P, NQ], U32, name="q_codes", align_bytes=64)
-        q_scales = sb.tile([P, NQ], U8, name="q_scales", align_bytes=64)
-        nc.scalar.copy(q_bf[:].rearrange("p (c i t) -> p c t i", i=4, t=4), q_raw[:].rearrange("p t (c i) -> p c t i", i=4))
+        q_bf = [sb.tile([P, P * 4], BF16, name="q_bf%d" % h, align_bytes=64) for h in range(2)]
+        q_codes = [sb.tile([P, P], U32, name="q_codes%d" % h, align_bytes=64) for h in range(2)]
+        q_scales = [sb.tile([P, P], U8, name="q_scales%d" % h, align_bytes=64) for h in range(2)]
+        for h in range(2):
+            nc.scalar.copy(q_bf[h][:].rearrange("p (c i t) -> p c t i", i=4, t=4), q_raw[h][:].rearrange("p t (c i) -> p c t i", i=4))
         neg_ls = sb.tile([P, 2], F32, name="neg_ls")
-        nc.scalar.mul(neg_ls[:], ls_col[:], -1.0)
+        nc.gpsimd.tensor_scalar(neg_ls[:], ls_col[:], -1.0, 0.0, MULT, ADD)
 
         yT = [sb.tile([P, 4, P], F32, name="yT%d" % h) for h in range(2)]
         for a in range(4):
@@ -93,25 +111,37 @@ def tile_attend_plw_rope_f_topk_kernel(tc, qT, kT, cT, wT, ls, offs, offs2, out_
             u_bf = sb.tile([P, P * 4], BF16, name="u_bf%d" % a, align_bytes=64)
             u_codes = sb.tile([P, P], U32, name="u_codes%d" % a, align_bytes=64)
             u_scales = sb.tile([P, P], U8, name="u_scales%d" % a, align_bytes=64)
+            product(prod_odd[:, 2:4, :], kg[3], trig[1][:, 0:2, :], cols)
+            pairs = words[a]
             nc.vector.tensor_tensor(
-                u_bf[:].rearrange("p (c i t) -> p c t i", i=4, t=4),
-                prod_even[:, :, cols].rearrange("p t (c i) -> p c t i", i=4),
-                prod_odd[:, :, cols].rearrange("p t (c i) -> p c t i", i=4),
+                pairs[:, 1, :].bitcast(BF16).rearrange("p (c i e) -> p c e i", i=4, e=2),
+                prod_even[:, 2:4, cols].rearrange("p e (c i) -> p c e i", i=4),
+                prod_odd[:, 2:4, cols].rearrange("p e (c i) -> p c e i", i=4),
                 ADD,
             )
+            if a < 2:
+                nc.scalar.copy(u_bf[:].bitcast(F32).rearrange("p (n u) -> p n u", u=2), pairs[:].rearrange("p u n -> p n u"))
+            else:
+                nc.vector.tensor_copy(
+                    u_bf[:].bitcast(I32).rearrange("p (n u) -> p n u", u=2), pairs[:].bitcast(I32).rearrange("p u n -> p n u")
+                )
             if a == 0:
-                nc.vector.quantize_mx(out=q_codes[:].bitcast(FP8X4), scales=q_scales[:], in_=q_bf[:])
+                for h in range(2):
+                    nc.vector.quantize_mx(out=q_codes[h][:].bitcast(FP8X4), scales=q_scales[h][:], in_=q_bf[h][:])
             nc.vector.quantize_mx(out=u_codes[:].bitcast(FP8X4), scales=u_scales[:], in_=u_bf[:])
-            score = ps.tile([P, 2, P], F32, name="score%d" % a)
+            if a < 2:
+                score = [ps.tile([P, P], F32, name="score%d%d" % (a, h))[:] for h in range(2)]
+            else:
+                both = ps.tile([P, 2, P], F32, name="score%d" % a, tag="late%d" % (a - 2))
+                score = [both[:, h, :] for h in range(2)]
             for h in range(2):
-                qs = slice(h * P, (h + 1) * P)
                 nc.tensor.matmul_mx(
-                    out=score[:, h, :], lhsT=q_codes[:, qs].bitcast(FP8X4), lhsT_scale=q_scales[:, qs],
+                    out=score[h], lhsT=q_codes[h][:].bitcast(FP8X4), lhsT_scale=q_scales[h][:],
                     rhs=u_codes[:].bitcast(FP8X4), rhs_scale=u_scales[:], start=True, stop=True,
                 )
             for h in range(2):
                 nc.scalar.activation(
-                    yT[h][:, :, a * 32 : (a + 1) * 32], score[:, h, :].rearrange("p (s r) -> p r s", r=4), EXP, bias=neg_ls[:, h : h + 1]
+                    yT[h][:, :, a * 32 : (a + 1) * 32], score[h].rearrange("p (s r) -> p r s", r=4), EXP, bias=neg_ls[:, h : h + 1]
                 )
 
         y = [sb.tile([P, 4, P], F32, name="y%d" % h) for h in range(2)]
@@ -119,17 +149,20 @@ def tile_attend_plw_rope_f_topk_kernel(tc, qT, kT, cT, wT, ls, offs, offs2, out_
         y_codes = sb.tile([P, NQ], U32, name="y_codes", align_bytes=64)
         y_scales = sb.tile([P, NQ], U8, name="y_scales", align_bytes=64)
         out_rows = out_0.rearrange("(p r) q -> p r q", r=4)
-        turned = [ps.tile([P, 4, P], F32, name="turned%d" % h) for h in range(2)]
+        turned = [ps.tile([P, 4, P], F32, name="turned%d" % h, tag="turned%d" % h) for h in range(2)]
         for h in range(2):
             for r in range(4):
                 nc.tensor.transpose(turned[h][:, r, :], yT[h][:, r, :], ident[:])
         for h in range(2):
             qs = slice(h * P, (h + 1) * P)
             nc.vector.tensor_copy(y_bf[h][:].rearrange("p (q r) -> p q r", r=4), turned[h][:].rearrange("p r q -> p q r"))
-            other = 1 - h
-            nc.scalar.copy(y[other][:], turned[other][:])
-            queue = nc.sync if h == 0 else nc.scalar
-            queue.dma_start(out_rows[:, :, other * P : (other + 1) * P], y[other][:])
+            if h == 0:
+                nc.scalar.copy(y[h][:], turned[h][:])
+                nc.sync.dma_start(out_rows[:, :, qs], y[h][:])
+            else:
+                for rs, queue in ((slice(0, 2), nc.sync), (slice(2, 4), nc.scalar)):
+                    nc.scalar.copy(y[h][:, rs, :], turned[h][:, rs, :])
+                    queue.dma_start(out_rows[:, rs, qs], y[h][:, rs, :])
             nc.vector.quantize_mx(out=y_codes[:, qs].bitcast(FP8X4), scales=y_scales[:, qs], in_=y_bf[h][:])
         nc.sync.dma_start(out_1[0].rearrange("p q x -> p (q x)").bitcast(I32), y_codes[:].bitcast(I32))
         for quad in range(4):

@@ -36,8 +36,8 @@ def tile_attend_plw_rope_f_topk_kernel(tc, qT, kT, cT, wT, ls, offs, offs2, out_
         k_win = [sb.tile([P, T], F32, name="k_win%d" % t) for t in range(4)]
         c_win = [sb.tile([P, NPOS], F32, name="c_win%d" % j) for j in range(2)]
         w_win = [sb.tile([P, NPOS], F32, name="w_win%d" % j) for j in range(2)]
-        q_raw = [sb.tile([P, 4, P], F32, name="q_raw%d" % h) for h in range(2)]
-        ls_col = sb.tile([P, 2], F32, name="ls_col")
+        q_raw = sb.tile([P, 4, NQ], F32, name="q_raw")
+        ls_rows = sb.tile([P, P], F32, name="ls_rows")
 
         nc.sync.dma_start(c_win[0][:], c_rows[:, 0, :])
         nc.sync.dma_start(pos[:], offs2)
@@ -49,15 +49,16 @@ def tile_attend_plw_rope_f_topk_kernel(tc, qT, kT, cT, wT, ls, offs, offs2, out_
         nc.sync.dma_start(w_win[1][:], w_rows[:, 2, :])
         nc.sync.dma_start(k_win[2][:], k_rows[:, 2, :])
         nc.sync.dma_start(k_win[3][:], k_rows[:, 3, :])
-        for h in range(2):
-            nc.sync.dma_start(q_raw[h][:], qT[0].rearrange("(p t) n -> p t n", t=4)[:, :, h * P : (h + 1) * P])
-        with nc.allow_non_contiguous_dma(reason="one log-sum-exp to a partition"):
-            nc.sync.dma_start(ls_col[:], ls[0, 0, :].rearrange("(h p) -> p h", p=P))
+        nc.sync.dma_start(q_raw[:], qT[0].rearrange("(p t) n -> p t n", t=4))
+        nc.vector.memset(ls_rows[:], 0.0)
+        nc.scalar.dma_start(ls_rows[0:2, :], ls[0, 0, :].rearrange("(h p) -> h p", p=P))
 
         ident = sb.tile([P, P], F32, name="ident")
         make_identity(nc, ident[:])
-        warm = sb.tile([P, 1], F32, name="warm")
-        nc.scalar.activation(warm[:], ident[:, 0:1], EXP)
+        ls_cols = ps.tile([P, P], F32, name="ls_cols", tag="turned1")
+        nc.tensor.transpose(ls_cols[:], ls_rows[:], ident[:])
+        neg_ls = sb.tile([P, 2], F32, name="neg_ls")
+        nc.scalar.mul(neg_ls[:], ls_cols[:, 0:2], -1.0)
 
         prod_even = sb.tile([P, 4, N], F32, name="prod_even")
         prod_odd = sb.tile([P, 4, N], F32, name="prod_odd")
@@ -100,49 +101,57 @@ def tile_attend_plw_rope_f_topk_kernel(tc, qT, kT, cT, wT, ls, offs, offs2, out_
         q_bf = [sb.tile([P, P * 4], BF16, name="q_bf%d" % h, align_bytes=64) for h in range(2)]
         q_codes = [sb.tile([P, P], U32, name="q_codes%d" % h, align_bytes=64) for h in range(2)]
         q_scales = [sb.tile([P, P], U8, name="q_scales%d" % h, align_bytes=64) for h in range(2)]
-        for h in range(2):
-            nc.scalar.copy(q_bf[h][:].rearrange("p (c i t) -> p c t i", i=4, t=4), q_raw[h][:].rearrange("p t (c i) -> p c t i", i=4))
-        neg_ls = sb.tile([P, 2], F32, name="neg_ls")
-        nc.gpsimd.tensor_scalar(neg_ls[:], ls_col[:], -1.0, 0.0, MULT, ADD)
+
+        def quantize_queries(h):
+            nc.scalar.copy(q_bf[h][:].rearrange("p (n t) -> p n t", t=4), q_raw[:, :, h * P : (h + 1) * P].rearrange("p t n -> p n t"))
+            nc.vector.quantize_mx(out=q_codes[h][:].bitcast(FP8X4), scales=q_scales[h][:], in_=q_bf[h][:])
+
+        quantize_queries(0)
 
         yT = [sb.tile([P, 4, P], F32, name="yT%d" % h) for h in range(2)]
-        for a in range(4):
-            cols = slice(a * P, (a + 1) * P)
-            u_bf = sb.tile([P, P * 4], BF16, name="u_bf%d" % a, align_bytes=64)
-            u_codes = sb.tile([P, P], U32, name="u_codes%d" % a, align_bytes=64)
-            u_scales = sb.tile([P, P], U8, name="u_scales%d" % a, align_bytes=64)
+        u_codes = [sb.tile([P, P], U32, name="u_codes%d" % c, align_bytes=64) for c in range(4)]
+        u_scales = [sb.tile([P, P], U8, name="u_scales%d" % c, align_bytes=64) for c in range(4)]
+
+        def quantize_keys(c):
+            cols = slice(c * P, (c + 1) * P)
+            u_bf = sb.tile([P, P * 4], BF16, name="u_bf%d" % c, align_bytes=64)
             product(prod_odd[:, 2:4, :], kg[3], trig[1][:, 0:2, :], cols)
-            pairs = words[a]
             nc.vector.tensor_tensor(
-                pairs[:, 1, :].bitcast(BF16).rearrange("p (c i e) -> p c e i", i=4, e=2),
+                words[c][:, 1, :].bitcast(BF16).rearrange("p (c i e) -> p c e i", i=4, e=2),
                 prod_even[:, 2:4, cols].rearrange("p e (c i) -> p c e i", i=4),
                 prod_odd[:, 2:4, cols].rearrange("p e (c i) -> p c e i", i=4),
                 ADD,
             )
-            if a < 2:
-                nc.scalar.copy(u_bf[:].bitcast(F32).rearrange("p (n u) -> p n u", u=2), pairs[:].rearrange("p u n -> p n u"))
+            if c < 2:
+                nc.scalar.copy(u_bf[:].bitcast(F32).rearrange("p (n u) -> p n u", u=2), words[c][:].rearrange("p u n -> p n u"))
             else:
-                nc.vector.tensor_copy(
-                    u_bf[:].bitcast(I32).rearrange("p (n u) -> p n u", u=2), pairs[:].bitcast(I32).rearrange("p u n -> p n u")
-                )
-            if a == 0:
-                for h in range(2):
-                    nc.vector.quantize_mx(out=q_codes[h][:].bitcast(FP8X4), scales=q_scales[h][:], in_=q_bf[h][:])
-            nc.vector.quantize_mx(out=u_codes[:].bitcast(FP8X4), scales=u_scales[:], in_=u_bf[:])
-            if a < 2:
-                score = [ps.tile([P, P], F32, name="score%d%d" % (a, h))[:] for h in range(2)]
-            else:
-                both = ps.tile([P, 2, P], F32, name="score%d" % a, tag="late%d" % (a - 2))
-                score = [both[:, h, :] for h in range(2)]
+                nc.vector.tensor_copy(u_bf[:].bitcast(I32).rearrange("p (n u) -> p n u", u=2), words[c][:].bitcast(I32).rearrange("p u n -> p n u"))
+            nc.vector.quantize_mx(out=u_codes[c][:].bitcast(FP8X4), scales=u_scales[c][:], in_=u_bf[:])
+
+        def scores(c, h, bank):
+            nc.tensor.matmul_mx(
+                out=bank, lhsT=q_codes[h][:].bitcast(FP8X4), lhsT_scale=q_scales[h][:],
+                rhs=u_codes[c][:].bitcast(FP8X4), rhs_scale=u_scales[c][:], start=True, stop=True,
+            )
+
+        def weights(c, h, bank):
+            nc.scalar.activation(yT[h][:, :, c * 32 : (c + 1) * 32], bank.rearrange("p (s r) -> p r s", r=4), EXP, bias=neg_ls[:, h : h + 1])
+
+        for c in range(2):
+            quantize_keys(c)
+        quantize_queries(1)
+        for h in range(2):
+            for c in range(2):
+                bank = ps.tile([P, P], F32, name="score%d%d" % (c, h))
+                scores(c, h, bank[:])
+                weights(c, h, bank[:])
+        for c in range(2, 4):
+            quantize_keys(c)
+            both = ps.tile([P, 2, P], F32, name="score%d" % c, tag="late%d" % (c - 2))
             for h in range(2):
-                nc.tensor.matmul_mx(
-                    out=score[h], lhsT=q_codes[h][:].bitcast(FP8X4), lhsT_scale=q_scales[h][:],
-                    rhs=u_codes[:].bitcast(FP8X4), rhs_scale=u_scales[:], start=True, stop=True,
-                )
+                scores(c, h, both[:, h, :])
             for h in range(2):
-                nc.scalar.activation(
-                    yT[h][:, :, a * 32 : (a + 1) * 32], score[h].rearrange("p (s r) -> p r s", r=4), EXP, bias=neg_ls[:, h : h + 1]
-                )
+                weights(c, h, both[:, h, :])
 
         y = [sb.tile([P, 4, P], F32, name="y%d" % h) for h in range(2)]
         y_bf = [sb.tile([P, P * 4], BF16, name="y_bf%d" % h, align_bytes=64) for h in range(2)]
@@ -155,11 +164,12 @@ def tile_attend_plw_rope_f_topk_kernel(tc, qT, kT, cT, wT, ls, offs, offs2, out_
                 nc.tensor.transpose(turned[h][:, r, :], yT[h][:, r, :], ident[:])
         for h in range(2):
             qs = slice(h * P, (h + 1) * P)
-            nc.vector.tensor_copy(y_bf[h][:].rearrange("p (q r) -> p q r", r=4), turned[h][:].rearrange("p r q -> p q r"))
             if h == 0:
                 nc.scalar.copy(y[h][:], turned[h][:])
                 nc.sync.dma_start(out_rows[:, :, qs], y[h][:])
+                nc.vector.tensor_copy(y_bf[h][:].rearrange("p (q r) -> p q r", r=4), y[h][:].rearrange("p r q -> p q r"))
             else:
+                nc.vector.tensor_copy(y_bf[h][:].rearrange("p (q r) -> p q r", r=4), turned[h][:].rearrange("p r q -> p q r"))
                 for rs, queue in ((slice(0, 2), nc.sync), (slice(2, 4), nc.scalar)):
                     nc.scalar.copy(y[h][:, rs, :], turned[h][:, rs, :])
                     queue.dma_start(out_rows[:, rs, qs], y[h][:, rs, :])

@@ -16,6 +16,7 @@ U8 = mybir.dt.uint8
 FP8X4 = mybir.dt.float8_e4m3fn_x4
 MULT = mybir.AluOpType.mult
 ADD = mybir.AluOpType.add
+SUB = mybir.AluOpType.subtract
 EXP = mybir.ActivationFunctionType.Exp
 
 P = 128
@@ -55,10 +56,15 @@ def tile_attend_plw_rope_f_topk_kernel(tc, qT, kT, cT, wT, ls, offs, offs2, out_
 
         ident = sb.tile([P, P], F32, name="ident")
         make_identity(nc, ident[:])
-        ls_cols = ps.tile([P, P], F32, name="ls_cols", tag="turned1")
-        nc.tensor.transpose(ls_cols[:], ls_rows[:], ident[:])
-        neg_ls = sb.tile([P, 2], F32, name="neg_ls")
-        nc.scalar.mul(neg_ls[:], ls_cols[:, 0:2], -1.0)
+        ls_cols_ps = ps.tile([P, P], F32, name="ls_cols_ps", tag="score0")
+        nc.tensor.transpose(ls_cols_ps[:], ls_rows[:], ident[:])
+        ls_cols = sb.tile([P, 2], F32, name="ls_cols")
+        nc.scalar.copy(ls_cols[:], ls_cols_ps[:, 0:2])
+        ls_wide_ps = ps.tile([P, 2, P], F32, name="ls_wide_ps", tag="score1")
+        for h in range(2):
+            nc.tensor.transpose(ls_wide_ps[:, h, :], ls_cols[:, h : h + 1].to_broadcast([P, P]), ident[:])
+        ls_wide = sb.tile([P, NQ], F32, name="ls_wide")
+        nc.scalar.copy(ls_wide[:], ls_wide_ps[:].rearrange("p h q -> p (h q)"))
 
         prod_even = sb.tile([P, 4, N], F32, name="prod_even")
         prod_odd = sb.tile([P, 4, N], F32, name="prod_odd")
@@ -69,7 +75,8 @@ def tile_attend_plw_rope_f_topk_kernel(tc, qT, kT, cT, wT, ls, offs, offs2, out_
             width = cols.stop - cols.start
             nc.vector.tensor_tensor(dst[:, :, cols], key[:, cols].unsqueeze(1).to_broadcast([P, 2, width]), factors[:, :, cols], MULT)
 
-        words = [sb.tile([P, 2, P], F32, name="words%d" % c) for c in range(4)]
+        chunks = [slice(0, 256), slice(256, 384), slice(384, 512)]
+        words = [sb.tile([P, 2, c.stop - c.start], F32, name="words%d" % c.start) for c in chunks]
         halves = [slice(0, HALF), slice(HALF, N)]
         for j in range(2):
             nc.vector.tensor_copy(trig[j][:, 1, :], c_win[j][:].indirect(pos[:]))
@@ -95,84 +102,62 @@ def tile_attend_plw_rope_f_topk_kernel(tc, qT, kT, cT, wT, ls, offs, offs2, out_
                     nc.scalar.copy(rounded[:].rearrange("s b (p e) -> s b p e", e=2), summed[:].rearrange("s b e p -> s b p e"))
                     for b in range(2):
                         nc.tensor.transpose(back[:, 2 * a + b, :], rounded[:, b, :].bitcast(F32), ident[:])
-                for c in range(4):
-                    nc.scalar.copy(words[c][:, 0, :], back[:, c, :])
+                back_row = back[:].rearrange("p c s -> p (c s)")
+                for c, cols in enumerate(chunks):
+                    nc.scalar.copy(words[c][:, 0, :], back_row[:, cols])
 
-        q_bf = [sb.tile([P, P * 4], BF16, name="q_bf%d" % h, align_bytes=64) for h in range(2)]
-        q_codes = [sb.tile([P, P], U32, name="q_codes%d" % h, align_bytes=64) for h in range(2)]
-        q_scales = [sb.tile([P, P], U8, name="q_scales%d" % h, align_bytes=64) for h in range(2)]
+        q_bf = sb.tile([P, NQ * 4], BF16, name="q_bf", align_bytes=64)
+        q_codes = sb.tile([P, NQ], U32, name="q_codes", align_bytes=64)
+        q_scales = sb.tile([P, NQ], U8, name="q_scales", align_bytes=64)
+        nc.scalar.copy(q_bf[:].rearrange("p (c i t) -> p c t i", i=4, t=4), q_raw[:].rearrange("p t (c i) -> p c t i", i=4))
 
-        def quantize_queries(h):
-            nc.scalar.copy(q_bf[h][:].rearrange("p (n t) -> p n t", t=4), q_raw[:, :, h * P : (h + 1) * P].rearrange("p t n -> p n t"))
-            nc.vector.quantize_mx(out=q_codes[h][:].bitcast(FP8X4), scales=q_scales[h][:], in_=q_bf[h][:])
-
-        quantize_queries(0)
-
-        yT = [sb.tile([P, 4, P], F32, name="yT%d" % h) for h in range(2)]
-        u_codes = [sb.tile([P, P], U32, name="u_codes%d" % c, align_bytes=64) for c in range(4)]
-        u_scales = [sb.tile([P, P], U8, name="u_scales%d" % c, align_bytes=64) for c in range(4)]
-
-        def quantize_keys(c):
-            cols = slice(c * P, (c + 1) * P)
-            u_bf = sb.tile([P, P * 4], BF16, name="u_bf%d" % c, align_bytes=64)
+        for cols in halves:
             product(prod_odd[:, 2:4, :], kg[3], trig[1][:, 0:2, :], cols)
+        u_bf = sb.tile([P, 4, P * 4], BF16, name="u_bf", align_bytes=64)
+        u_words = u_bf[:].bitcast(F32).rearrange("p r (s u) -> p s r u", u=2)
+        for c, cols in enumerate(chunks):
             nc.vector.tensor_tensor(
                 words[c][:, 1, :].bitcast(BF16).rearrange("p (c i e) -> p c e i", i=4, e=2),
                 prod_even[:, 2:4, cols].rearrange("p e (c i) -> p c e i", i=4),
                 prod_odd[:, 2:4, cols].rearrange("p e (c i) -> p c e i", i=4),
                 ADD,
             )
+        nc.vector.quantize_mx(out=q_codes[:].bitcast(FP8X4), scales=q_scales[:], in_=q_bf[:])
+        for c, cols in enumerate(chunks):
+            dst = u_words[:, cols.start // 4 : cols.stop // 4]
+            src = words[c][:].rearrange("p u (s r) -> p s r u", r=4)
             if c < 2:
-                nc.scalar.copy(u_bf[:].bitcast(F32).rearrange("p (n u) -> p n u", u=2), words[c][:].rearrange("p u n -> p n u"))
+                nc.scalar.copy(dst, src)
             else:
-                nc.vector.tensor_copy(u_bf[:].bitcast(I32).rearrange("p (n u) -> p n u", u=2), words[c][:].bitcast(I32).rearrange("p u n -> p n u"))
-            nc.vector.quantize_mx(out=u_codes[c][:].bitcast(FP8X4), scales=u_scales[c][:], in_=u_bf[:])
+                nc.vector.tensor_copy(dst, src)
 
-        def scores(c, h, bank):
+        u_codes = [sb.tile([P, P], U32, name="u_codes%d" % r, align_bytes=64) for r in range(4)]
+        u_scales = [sb.tile([P, P], U8, name="u_scales%d" % r, align_bytes=64) for r in range(4)]
+        score = [ps.tile([P, NQ], F32, name="score%d" % r, tag="score%d" % r) for r in range(4)]
+        for r in range(4):
+            nc.vector.quantize_mx(out=u_codes[r][:].bitcast(FP8X4), scales=u_scales[r][:], in_=u_bf[:, r, :])
             nc.tensor.matmul_mx(
-                out=bank, lhsT=q_codes[h][:].bitcast(FP8X4), lhsT_scale=q_scales[h][:],
-                rhs=u_codes[c][:].bitcast(FP8X4), rhs_scale=u_scales[c][:], start=True, stop=True,
+                out=score[r][:], lhsT=u_codes[r][:].bitcast(FP8X4), lhsT_scale=u_scales[r][:],
+                rhs=q_codes[:].bitcast(FP8X4), rhs_scale=q_scales[:], start=True, stop=True,
             )
 
-        def weights(c, h, bank):
-            nc.scalar.activation(yT[h][:, :, c * 32 : (c + 1) * 32], bank.rearrange("p (s r) -> p r s", r=4), EXP, bias=neg_ls[:, h : h + 1])
+        y = sb.tile([P, 4, NQ], F32, name="y")
+        out_rows = out_0.rearrange("(p r) q -> p r q", r=4)
+        for r in range(4):
+            shifted = sb.tile([P, NQ], F32, name="shifted%d" % r)
+            nc.vector.tensor_tensor(shifted[:], score[r][:], ls_wide[:], SUB)
+            nc.scalar.activation(y[:, r, :], shifted[:], EXP)
+            if r % 2 == 1:
+                nc.sync.dma_start(out_rows[:, r - 1 : r + 1, :], y[:, r - 1 : r + 1, :])
 
-        for c in range(2):
-            quantize_keys(c)
-        quantize_queries(1)
-        for h in range(2):
-            for c in range(2):
-                bank = ps.tile([P, P], F32, name="score%d%d" % (c, h))
-                scores(c, h, bank[:])
-                weights(c, h, bank[:])
-        for c in range(2, 4):
-            quantize_keys(c)
-            both = ps.tile([P, 2, P], F32, name="score%d" % c, tag="late%d" % (c - 2))
-            for h in range(2):
-                scores(c, h, both[:, h, :])
-            for h in range(2):
-                weights(c, h, both[:, h, :])
-
-        y = [sb.tile([P, 4, P], F32, name="y%d" % h) for h in range(2)]
         y_bf = [sb.tile([P, P * 4], BF16, name="y_bf%d" % h, align_bytes=64) for h in range(2)]
         y_codes = sb.tile([P, NQ], U32, name="y_codes", align_bytes=64)
         y_scales = sb.tile([P, NQ], U8, name="y_scales", align_bytes=64)
-        out_rows = out_0.rearrange("(p r) q -> p r q", r=4)
-        turned = [ps.tile([P, 4, P], F32, name="turned%d" % h, tag="turned%d" % h) for h in range(2)]
-        for h in range(2):
-            for r in range(4):
-                nc.tensor.transpose(turned[h][:, r, :], yT[h][:, r, :], ident[:])
         for h in range(2):
             qs = slice(h * P, (h + 1) * P)
-            if h == 0:
-                nc.scalar.copy(y[h][:], turned[h][:])
-                nc.sync.dma_start(out_rows[:, :, qs], y[h][:])
-                nc.vector.tensor_copy(y_bf[h][:].rearrange("p (q r) -> p q r", r=4), y[h][:].rearrange("p r q -> p q r"))
-            else:
-                nc.vector.tensor_copy(y_bf[h][:].rearrange("p (q r) -> p q r", r=4), turned[h][:].rearrange("p r q -> p q r"))
-                for rs, queue in ((slice(0, 2), nc.sync), (slice(2, 4), nc.scalar)):
-                    nc.scalar.copy(y[h][:, rs, :], turned[h][:, rs, :])
-                    queue.dma_start(out_rows[:, rs, qs], y[h][:, rs, :])
+            nc.vector.tensor_copy(y_bf[h][:].rearrange("p (c i r) -> p c r i", i=4, r=4), y[:, :, qs].rearrange("p r (c i) -> p c r i", i=4))
+        for h in range(2):
+            qs = slice(h * P, (h + 1) * P)
             nc.vector.quantize_mx(out=y_codes[:, qs].bitcast(FP8X4), scales=y_scales[:, qs], in_=y_bf[h][:])
         nc.sync.dma_start(out_1[0].rearrange("p q x -> p (q x)").bitcast(I32), y_codes[:].bitcast(I32))
         for quad in range(4):

@@ -21,6 +21,7 @@ EXP = mybir.ActivationFunctionType.Exp
 
 P = 128
 HALF = N // 2
+POOL_SLOTS = 128
 
 
 def tile_attend_plw_rope_f_topk_kernel(tc, qT, kT, cT, wT, ls, offs, offs2, out_0, out_1, out_2):
@@ -44,10 +45,10 @@ def tile_attend_plw_rope_f_topk_kernel(tc, qT, kT, cT, wT, ls, offs, offs2, out_
         nc.sync.dma_start(pos[:], offs2)
         nc.sync.dma_start(w_win[0][:], w_rows[:, 0, :])
         nc.sync.dma_start(tok[:], offs)
-        nc.sync.dma_start(k_win[0][:], k_rows[:, 0, :])
-        nc.sync.dma_start(k_win[1][:], k_rows[:, 1, :])
         nc.sync.dma_start(c_win[1][:], c_rows[:, 2, :])
         nc.sync.dma_start(w_win[1][:], w_rows[:, 2, :])
+        nc.sync.dma_start(k_win[0][:], k_rows[:, 0, :])
+        nc.sync.dma_start(k_win[1][:], k_rows[:, 1, :])
         nc.sync.dma_start(k_win[2][:], k_rows[:, 2, :])
         nc.sync.dma_start(k_win[3][:], k_rows[:, 3, :])
         nc.sync.dma_start(q_raw[:], qT[0].rearrange("(p t) n -> p t n", t=4))
@@ -71,9 +72,10 @@ def tile_attend_plw_rope_f_topk_kernel(tc, qT, kT, cT, wT, ls, offs, offs2, out_
         trig = [sb.tile([P, 3, N], F32, name="trig%d" % j) for j in range(2)]
         kg = [sb.tile([P, N], F32, name="kg%d" % t) for t in range(4)]
 
-        def product(dst, key, factors, cols):
-            width = cols.stop - cols.start
-            nc.vector.tensor_tensor(dst[:, :, cols], key[:, cols].unsqueeze(1).to_broadcast([P, 2, width]), factors[:, :, cols], MULT)
+        def product(dst, key, factors):
+            for engine, cols in ((nc.gpsimd, slice(0, POOL_SLOTS)), (nc.vector, slice(POOL_SLOTS, HALF)), (nc.vector, slice(HALF, N))):
+                width = cols.stop - cols.start
+                engine.tensor_tensor(dst[:, :, cols], key[:, cols].unsqueeze(1).to_broadcast([P, 2, width]), factors[:, :, cols], MULT)
 
         chunks = [slice(0, 256), slice(256, 384), slice(384, 512)]
         words = [sb.tile([P, 2, c.stop - c.start], F32, name="words%d" % c.start) for c in chunks]
@@ -82,13 +84,13 @@ def tile_attend_plw_rope_f_topk_kernel(tc, qT, kT, cT, wT, ls, offs, offs2, out_
             nc.vector.tensor_copy(trig[j][:, 1, :], c_win[j][:].indirect(pos[:]))
             nc.vector.tensor_copy(trig[j][:, 2, :], w_win[j][:].indirect(pos[:]))
             nc.scalar.mul(trig[j][:, 0, :], trig[j][:, 2, :], -1.0)
+        for j in range(2):
             pair = slice(2 * j, 2 * j + 2)
             for t, dst, factors in ((2 * j, prod_even, trig[j][:, 1:3, :]), (2 * j + 1, prod_odd, trig[j][:, 0:2, :])):
                 for cols in halves:
                     nc.vector.tensor_copy(kg[t][:, cols], k_win[t][:].indirect(tok[:, cols.start // 16 : cols.stop // 16]))
                 if t < 3:
-                    for cols in halves:
-                        product(dst[:, pair, :], kg[t], factors, cols)
+                    product(dst[:, pair, :], kg[t], factors)
             if j == 0:
                 back = ps.tile([P, 4, P], F32, name="back", tag="turned0")
                 for a in range(2):
@@ -111,8 +113,7 @@ def tile_attend_plw_rope_f_topk_kernel(tc, qT, kT, cT, wT, ls, offs, offs2, out_
         q_scales = sb.tile([P, NQ], U8, name="q_scales", align_bytes=64)
         nc.scalar.copy(q_bf[:].rearrange("p (c i t) -> p c t i", i=4, t=4), q_raw[:].rearrange("p t (c i) -> p c t i", i=4))
 
-        for cols in halves:
-            product(prod_odd[:, 2:4, :], kg[3], trig[1][:, 0:2, :], cols)
+        product(prod_odd[:, 2:4, :], kg[3], trig[1][:, 0:2, :])
         u_bf = sb.tile([P, 4, P * 4], BF16, name="u_bf", align_bytes=64)
         u_words = u_bf[:].bitcast(F32).rearrange("p r (s u) -> p s r u", u=2)
         for c, cols in enumerate(chunks):
@@ -153,9 +154,10 @@ def tile_attend_plw_rope_f_topk_kernel(tc, qT, kT, cT, wT, ls, offs, offs2, out_
         y_bf = [sb.tile([P, P * 4], BF16, name="y_bf%d" % h, align_bytes=64) for h in range(2)]
         y_codes = sb.tile([P, NQ], U32, name="y_codes", align_bytes=64)
         y_scales = sb.tile([P, NQ], U8, name="y_scales", align_bytes=64)
-        for h in range(2):
-            qs = slice(h * P, (h + 1) * P)
-            nc.vector.tensor_copy(y_bf[h][:].rearrange("p (c i r) -> p c r i", i=4, r=4), y[:, :, qs].rearrange("p r (c i) -> p c r i", i=4))
+        for rs in (slice(0, 2), slice(2, 4)):
+            for h in range(2):
+                qs = slice(h * P, (h + 1) * P)
+                nc.vector.tensor_copy(y_bf[h][:].rearrange("p (c i r) -> p c r i", i=4, r=4)[:, :, rs], y[:, rs, qs].rearrange("p r (c i) -> p c r i", i=4))
         for h in range(2):
             qs = slice(h * P, (h + 1) * P)
             nc.vector.quantize_mx(out=y_codes[:, qs].bitcast(FP8X4), scales=y_scales[:, qs], in_=y_bf[h][:])

@@ -21,7 +21,6 @@ EXP = mybir.ActivationFunctionType.Exp
 
 P = 128
 HALF = N // 2
-POOL_SLOTS = 128
 
 
 def tile_attend_plw_rope_f_topk_kernel(tc, qT, kT, cT, wT, ls, offs, offs2, out_0, out_1, out_2):
@@ -38,7 +37,7 @@ def tile_attend_plw_rope_f_topk_kernel(tc, qT, kT, cT, wT, ls, offs, offs2, out_
         k_win = [sb.tile([P, T], F32, name="k_win%d" % t) for t in range(4)]
         c_win = [sb.tile([P, NPOS], F32, name="c_win%d" % j) for j in range(2)]
         w_win = [sb.tile([P, NPOS], F32, name="w_win%d" % j) for j in range(2)]
-        q_raw = sb.tile([P, 4, NQ], F32, name="q_raw")
+        q_raw = sb.tile([P, 4, NQ], F32, name="q_raw", tag="q_then_u", align_bytes=64)
         ls_rows = sb.tile([P, P], F32, name="ls_rows")
 
         nc.sync.dma_start(c_win[0][:], c_rows[:, 0, :])
@@ -57,44 +56,69 @@ def tile_attend_plw_rope_f_topk_kernel(tc, qT, kT, cT, wT, ls, offs, offs2, out_
 
         ident = sb.tile([P, P], F32, name="ident")
         make_identity(nc, ident[:])
-        ls_cols_ps = ps.tile([P, P], F32, name="ls_cols_ps", tag="score0")
-        nc.tensor.transpose(ls_cols_ps[:], ls_rows[:], ident[:])
-        ls_cols = sb.tile([P, 2], F32, name="ls_cols")
-        nc.scalar.copy(ls_cols[:], ls_cols_ps[:, 0:2])
-        ls_wide_ps = ps.tile([P, 2, P], F32, name="ls_wide_ps", tag="score1")
-        for h in range(2):
-            nc.tensor.transpose(ls_wide_ps[:, h, :], ls_cols[:, h : h + 1].to_broadcast([P, P]), ident[:])
-        ls_wide = sb.tile([P, NQ], F32, name="ls_wide")
-        nc.scalar.copy(ls_wide[:], ls_wide_ps[:].rearrange("p h q -> p (h q)"))
 
         prod_even = sb.tile([P, 4, N], F32, name="prod_even")
         prod_odd = sb.tile([P, 4, N], F32, name="prod_odd")
         trig = [sb.tile([P, 3, N], F32, name="trig%d" % j) for j in range(2)]
         kg = [sb.tile([P, N], F32, name="kg%d" % t) for t in range(4)]
 
-        def product(dst, key, factors):
-            for engine, cols in ((nc.gpsimd, slice(0, POOL_SLOTS)), (nc.vector, slice(POOL_SLOTS, HALF)), (nc.vector, slice(HALF, N))):
-                width = cols.stop - cols.start
-                engine.tensor_tensor(dst[:, :, cols], key[:, cols].unsqueeze(1).to_broadcast([P, 2, width]), factors[:, :, cols], MULT)
+        trig_ps = [[], []]
+
+        def product(t, dst, rows):
+            j = t // 2
+            if j == 0:
+                for cols in halves:
+                    nc.vector.tensor_tensor(dst[:, 0:2, cols], kg[t][:, cols].unsqueeze(1).to_broadcast([P, 2, HALF]), trig[0][:, rows, cols], MULT)
+                return
+            parts = [(nc.vector, b, trig_ps[j][b][:, rows, :]) for b in range(3)]
+            parts.insert(2, (nc.gpsimd, 3, trig[j][:, rows, 3 * P : 4 * P]))
+            for engine, b, factors in parts:
+                cols = slice(b * P, (b + 1) * P)
+                engine.tensor_tensor(dst[:, 2 * j : 2 * j + 2, cols], kg[t][:, cols].unsqueeze(1).to_broadcast([P, 2, P]), factors, MULT)
 
         chunks = [slice(0, 256), slice(256, 384), slice(384, 512)]
         words = [sb.tile([P, 2, c.stop - c.start], F32, name="words%d" % c.start) for c in chunks]
         halves = [slice(0, HALF), slice(HALF, N)]
+        last = slice(3 * P, 4 * P)
+        nc.vector.tensor_copy(trig[0][:, 1, :], c_win[0][:].indirect(pos[:]))
+        nc.vector.tensor_copy(trig[0][:, 2, :], w_win[0][:].indirect(pos[:]))
+        nc.scalar.mul(trig[0][:, 0, :], trig[0][:, 2, :], -1.0)
+        for j in (1,):
+            trig_ps[j].extend(ps.tile([P, 3, P], F32, name="trig_ps%d%d" % (j, b), tag="bank%d" % (3 * j + b)) for b in range(3))
+            for row, win in ((1, c_win[j]), (2, w_win[j])):
+                nc.vector.tensor_copy(trig[j][:, row, :], win[:].indirect(pos[:]))
+                by_slot_ps = ps.tile([P, 3, P], F32, name="by_slot_ps%d%d" % (j, row), tag="bank%d" % (5 + row))
+                for b in range(3):
+                    nc.tensor.transpose(by_slot_ps[:, b, :], trig[j][:, row, b * P : (b + 1) * P], ident[:])
+                for dst_row in ((1,) if row == 1 else (2, 0)):
+                    by_slot = sb.tile([P, 3, P], F32, name="by_slot%d%d" % (j, dst_row))
+                    if dst_row == 0:
+                        nc.scalar.mul(by_slot[:], by_slot_ps[:], -1.0)
+                    else:
+                        nc.scalar.copy(by_slot[:], by_slot_ps[:])
+                    for b in range(3):
+                        nc.tensor.transpose(trig_ps[j][b][:, dst_row, :], by_slot[:, b, :], ident[:])
+            nc.scalar.mul(trig[j][:, 0, last], trig[j][:, 2, last], -1.0)
+        ls_cols_ps = ps.tile([P, P], F32, name="ls_cols_ps", tag="bank7")
+        nc.tensor.transpose(ls_cols_ps[:], ls_rows[:], ident[:])
+        ls_cols = sb.tile([P, 2], F32, name="ls_cols")
+        nc.scalar.copy(ls_cols[:], ls_cols_ps[:, 0:2])
+        ls_wide_ps = ps.tile([P, 2, P], F32, name="ls_wide_ps", tag="bank6")
+        for h in range(2):
+            nc.tensor.transpose(ls_wide_ps[:, h, :], ls_cols[:, h : h + 1].to_broadcast([P, P]), ident[:])
+        ls_wide = sb.tile([P, NQ], F32, name="ls_wide")
+        nc.scalar.copy(ls_wide[:], ls_wide_ps[:].rearrange("p h q -> p (h q)"))
+
         for j in range(2):
-            nc.vector.tensor_copy(trig[j][:, 1, :], c_win[j][:].indirect(pos[:]))
-            nc.vector.tensor_copy(trig[j][:, 2, :], w_win[j][:].indirect(pos[:]))
-            nc.scalar.mul(trig[j][:, 0, :], trig[j][:, 2, :], -1.0)
-        for j in range(2):
-            pair = slice(2 * j, 2 * j + 2)
-            for t, dst, factors in ((2 * j, prod_even, trig[j][:, 1:3, :]), (2 * j + 1, prod_odd, trig[j][:, 0:2, :])):
+            for t, dst, rows in ((2 * j, prod_even, slice(1, 3)), (2 * j + 1, prod_odd, slice(0, 2))):
                 for cols in halves:
                     nc.vector.tensor_copy(kg[t][:, cols], k_win[t][:].indirect(tok[:, cols.start // 16 : cols.stop // 16]))
                 if t < 3:
-                    product(dst[:, pair, :], kg[t], factors)
+                    product(t, dst, rows)
             if j == 0:
-                back = ps.tile([P, 4, P], F32, name="back", tag="turned0")
+                back = ps.tile([P, 4, P], F32, name="back", tag="bank6")
                 for a in range(2):
-                    summed = ps.tile([P, 2, 2, P], F32, name="summed%d" % a, tag="late%d" % a)
+                    summed = ps.tile([P, 2, 2, P], F32, name="summed%d" % a, tag="bank%d" % a)
                     for b in range(2):
                         cols = slice((2 * a + b) * P, (2 * a + b + 1) * P)
                         for e in range(2):
@@ -113,8 +137,8 @@ def tile_attend_plw_rope_f_topk_kernel(tc, qT, kT, cT, wT, ls, offs, offs2, out_
         q_scales = sb.tile([P, NQ], U8, name="q_scales", align_bytes=64)
         nc.scalar.copy(q_bf[:].rearrange("p (c i t) -> p c t i", i=4, t=4), q_raw[:].rearrange("p t (c i) -> p c t i", i=4))
 
-        product(prod_odd[:, 2:4, :], kg[3], trig[1][:, 0:2, :])
-        u_bf = sb.tile([P, 4, P * 4], BF16, name="u_bf", align_bytes=64)
+        product(3, prod_odd, slice(0, 2))
+        u_bf = sb.tile([P, 4, P * 4], BF16, name="u_bf", tag="q_then_u", align_bytes=64)
         u_words = u_bf[:].bitcast(F32).rearrange("p r (s u) -> p s r u", u=2)
         for c, cols in enumerate(chunks):
             nc.vector.tensor_tensor(
@@ -123,7 +147,12 @@ def tile_attend_plw_rope_f_topk_kernel(tc, qT, kT, cT, wT, ls, offs, offs2, out_
                 prod_odd[:, 2:4, cols].rearrange("p e (c i) -> p c e i", i=4),
                 ADD,
             )
-        nc.vector.quantize_mx(out=q_codes[:].bitcast(FP8X4), scales=q_scales[:], in_=q_bf[:])
+
+        def quantize_queries(h):
+            qs = slice(h * P, (h + 1) * P)
+            nc.vector.quantize_mx(out=q_codes[:, qs].bitcast(FP8X4), scales=q_scales[:, qs], in_=q_bf[:, h * 4 * P : (h + 1) * 4 * P])
+
+        quantize_queries(0)
         for c, cols in enumerate(chunks):
             dst = u_words[:, cols.start // 4 : cols.stop // 4]
             src = words[c][:].rearrange("p u (s r) -> p s r u", r=4)
@@ -131,10 +160,11 @@ def tile_attend_plw_rope_f_topk_kernel(tc, qT, kT, cT, wT, ls, offs, offs2, out_
                 nc.scalar.copy(dst, src)
             else:
                 nc.vector.tensor_copy(dst, src)
+        quantize_queries(1)
 
         u_codes = [sb.tile([P, P], U32, name="u_codes%d" % r, align_bytes=64) for r in range(4)]
         u_scales = [sb.tile([P, P], U8, name="u_scales%d" % r, align_bytes=64) for r in range(4)]
-        score = [ps.tile([P, NQ], F32, name="score%d" % r, tag="score%d" % r) for r in range(4)]
+        score = [ps.tile([P, NQ], F32, name="score%d" % r, tag="bank%d" % (0, 1, 2, 7)[r]) for r in range(4)]
         for r in range(4):
             nc.vector.quantize_mx(out=u_codes[r][:].bitcast(FP8X4), scales=u_scales[r][:], in_=u_bf[:, r, :])
             nc.tensor.matmul_mx(

@@ -60,30 +60,24 @@ def tile_attend_plw_rope_f_topk_kernel(tc, qT, kT, cT, wT, ls, offs, offs2, out_
         prod_even = sb.tile([P, 4, N], F32, name="prod_even")
         prod_odd = sb.tile([P, 4, N], F32, name="prod_odd")
         trig = [sb.tile([P, 3, N], F32, name="trig%d" % j) for j in range(2)]
-        kg = [sb.tile([P, N], F32, name="kg%d" % t) for t in range(4)]
 
         trig_ps = [[], []]
 
-        def product(t, dst, rows):
+        def product(t, kg, dst, rows):
             j = t // 2
-            if j == 0:
-                for cols in halves:
-                    nc.vector.tensor_tensor(dst[:, 0:2, cols], kg[t][:, cols].unsqueeze(1).to_broadcast([P, 2, HALF]), trig[0][:, rows, cols], MULT)
-                return
             parts = [(nc.vector, b, trig_ps[j][b][:, rows, :]) for b in range(3)]
             parts.insert(2, (nc.gpsimd, 3, trig[j][:, rows, 3 * P : 4 * P]))
             for engine, b, factors in parts:
                 cols = slice(b * P, (b + 1) * P)
-                engine.tensor_tensor(dst[:, 2 * j : 2 * j + 2, cols], kg[t][:, cols].unsqueeze(1).to_broadcast([P, 2, P]), factors, MULT)
+                keys = kg[b // 2][:, (b % 2) * P : (b % 2 + 1) * P]
+                engine.tensor_tensor(dst[:, 2 * j : 2 * j + 2, cols], keys.unsqueeze(1).to_broadcast([P, 2, P]), factors, MULT)
 
         chunks = [slice(0, 256), slice(256, 384), slice(384, 512)]
         words = [sb.tile([P, 2, c.stop - c.start], F32, name="words%d" % c.start) for c in chunks]
         halves = [slice(0, HALF), slice(HALF, N)]
         last = slice(3 * P, 4 * P)
-        nc.vector.tensor_copy(trig[0][:, 1, :], c_win[0][:].indirect(pos[:]))
-        nc.vector.tensor_copy(trig[0][:, 2, :], w_win[0][:].indirect(pos[:]))
-        nc.scalar.mul(trig[0][:, 0, :], trig[0][:, 2, :], -1.0)
-        for j in (1,):
+        minus_sines = []
+        for j in (0, 1):
             trig_ps[j].extend(ps.tile([P, 3, P], F32, name="trig_ps%d%d" % (j, b), tag="bank%d" % (3 * j + b)) for b in range(3))
             for row, win in ((1, c_win[j]), (2, w_win[j])):
                 nc.vector.tensor_copy(trig[j][:, row, :], win[:].indirect(pos[:]))
@@ -96,48 +90,59 @@ def tile_attend_plw_rope_f_topk_kernel(tc, qT, kT, cT, wT, ls, offs, offs2, out_
                         nc.scalar.mul(by_slot[:], by_slot_ps[:], -1.0)
                     else:
                         nc.scalar.copy(by_slot[:], by_slot_ps[:])
+                    if dst_row == 0:
+                        minus_sines.append(by_slot)
+                        continue
                     for b in range(3):
                         nc.tensor.transpose(trig_ps[j][b][:, dst_row, :], by_slot[:, b, :], ident[:])
             nc.scalar.mul(trig[j][:, 0, last], trig[j][:, 2, last], -1.0)
-        ls_cols_ps = ps.tile([P, P], F32, name="ls_cols_ps", tag="bank7")
-        nc.tensor.transpose(ls_cols_ps[:], ls_rows[:], ident[:])
-        ls_cols = sb.tile([P, 2], F32, name="ls_cols")
-        nc.scalar.copy(ls_cols[:], ls_cols_ps[:, 0:2])
-        ls_wide_ps = ps.tile([P, 2, P], F32, name="ls_wide_ps", tag="bank6")
-        for h in range(2):
-            nc.tensor.transpose(ls_wide_ps[:, h, :], ls_cols[:, h : h + 1].to_broadcast([P, P]), ident[:])
-        ls_wide = sb.tile([P, NQ], F32, name="ls_wide")
-        nc.scalar.copy(ls_wide[:], ls_wide_ps[:].rearrange("p h q -> p (h q)"))
 
         for j in range(2):
             for t, dst, rows in ((2 * j, prod_even, slice(1, 3)), (2 * j + 1, prod_odd, slice(0, 2))):
-                for cols in halves:
-                    nc.vector.tensor_copy(kg[t][:, cols], k_win[t][:].indirect(tok[:, cols.start // 16 : cols.stop // 16]))
+                kg = [sb.tile([P, HALF], F32, name="kg%d%d" % (t, h)) for h in range(2)]
+                for h, cols in enumerate(halves):
+                    nc.vector.tensor_copy(kg[h][:], k_win[t][:].indirect(tok[:, cols.start // 16 : cols.stop // 16]))
                 if t < 3:
-                    product(t, dst, rows)
+                    product(t, kg, dst, rows)
+                if t % 2 == 0:
+                    for b in range(3):
+                        nc.tensor.transpose(trig_ps[j][b][:, 0, :], minus_sines[j][:, b, :], ident[:])
             if j == 0:
-                back = ps.tile([P, 4, P], F32, name="back", tag="bank6")
+                back = ps.tile([P, 4, P], F32, name="back", tag="bank0")
+                summed = [ps.tile([P, 2, 2, P], F32, name="summed%d" % a, tag="bank%d" % (6 + a)) for a in range(2)]
+                for o, src in enumerate((prod_even, prod_odd)):
+                    for a in range(2):
+                        for b in range(2):
+                            cols = slice((2 * a + b) * P, (2 * a + b + 1) * P)
+                            for e in range(2):
+                                first = o == 0 and b == 0 and e == 0
+                                final = o == 1 and b == 1 and e == 1
+                                nc.tensor.matmul(summed[a][:, b, e, :], src[:, e, cols], ident[:], start=first, stop=final, is_transpose=True)
                 for a in range(2):
-                    summed = ps.tile([P, 2, 2, P], F32, name="summed%d" % a, tag="bank%d" % a)
-                    for b in range(2):
-                        cols = slice((2 * a + b) * P, (2 * a + b + 1) * P)
-                        for e in range(2):
-                            nc.tensor.matmul(summed[:, b, e, :], prod_even[:, e, cols], ident[:], start=True, stop=False, is_transpose=True)
-                            nc.tensor.matmul(summed[:, b, e, :], prod_odd[:, e, cols], ident[:], start=False, stop=True, is_transpose=True)
                     rounded = sb.tile([P, 2, 2 * P], BF16, name="rounded%d" % a)
-                    nc.scalar.copy(rounded[:].rearrange("s b (p e) -> s b p e", e=2), summed[:].rearrange("s b e p -> s b p e"))
+                    nc.scalar.copy(rounded[:].rearrange("s b (p e) -> s b p e", e=2), summed[a][:].rearrange("s b e p -> s b p e"))
                     for b in range(2):
                         nc.tensor.transpose(back[:, 2 * a + b, :], rounded[:, b, :].bitcast(F32), ident[:])
                 back_row = back[:].rearrange("p c s -> p (c s)")
                 for c, cols in enumerate(chunks):
                     nc.scalar.copy(words[c][:, 0, :], back_row[:, cols])
 
+        ls_cols_ps = ps.tile([P, P], F32, name="ls_cols_ps", tag="bank1")
+        nc.tensor.transpose(ls_cols_ps[:], ls_rows[:], ident[:])
+        ls_cols = sb.tile([P, 2], F32, name="ls_cols")
+        nc.scalar.copy(ls_cols[:], ls_cols_ps[:, 0:2])
+        ls_wide_ps = ps.tile([P, 2, P], F32, name="ls_wide_ps", tag="bank2")
+        for h in range(2):
+            nc.tensor.transpose(ls_wide_ps[:, h, :], ls_cols[:, h : h + 1].to_broadcast([P, P]), ident[:])
+        ls_wide = sb.tile([P, NQ], F32, name="ls_wide")
+        nc.scalar.copy(ls_wide[:], ls_wide_ps[:].rearrange("p h q -> p (h q)"))
+
         q_bf = sb.tile([P, NQ * 4], BF16, name="q_bf", align_bytes=64)
         q_codes = sb.tile([P, NQ], U32, name="q_codes", align_bytes=64)
         q_scales = sb.tile([P, NQ], U8, name="q_scales", align_bytes=64)
         nc.scalar.copy(q_bf[:].rearrange("p (c i t) -> p c t i", i=4, t=4), q_raw[:].rearrange("p t (c i) -> p c t i", i=4))
 
-        product(3, prod_odd, slice(0, 2))
+        product(3, kg, prod_odd, slice(0, 2))
         u_bf = sb.tile([P, 4, P * 4], BF16, name="u_bf", tag="q_then_u", align_bytes=64)
         u_words = u_bf[:].bitcast(F32).rearrange("p r (s u) -> p s r u", u=2)
         for c, cols in enumerate(chunks):

@@ -72,7 +72,7 @@ def tile_attend_plw_rope_f_topk_kernel(tc, qT, kT, cT, wT, ls, offs, offs2, out_
                 keys = kg[b // 2][:, (b % 2) * P : (b % 2 + 1) * P]
                 engine.tensor_tensor(dst[:, 2 * j : 2 * j + 2, cols], keys.unsqueeze(1).to_broadcast([P, 2, P]), factors, MULT)
 
-        chunks = [slice(0, 256), slice(256, 384), slice(384, 512)]
+        chunks = [slice(0, 128), slice(128, 320), slice(320, 512)]
         words = [sb.tile([P, 2, c.stop - c.start], F32, name="words%d" % c.start) for c in chunks]
         halves = [slice(0, HALF), slice(HALF, N)]
         last = slice(3 * P, 4 * P)

@@ -18,6 +18,7 @@ MULT = mybir.AluOpType.mult
 ADD = mybir.AluOpType.add
 SUB = mybir.AluOpType.subtract
 EXP = mybir.ActivationFunctionType.Exp
+COPY = mybir.ActivationFunctionType.Copy
 
 P = 128
 HALF = N // 2
@@ -44,12 +45,11 @@ def tile_attend_plw_rope_f_topk_kernel(tc, qT, kT, cT, wT, ls, offs, offs2, out_
         nc.sync.dma_start(pos[:], offs2)
         nc.sync.dma_start(w_win[0][:], w_rows[:, 0, :])
         nc.sync.dma_start(tok[:], offs)
-        nc.sync.dma_start(c_win[1][:], c_rows[:, 2, :])
-        nc.sync.dma_start(w_win[1][:], w_rows[:, 2, :])
-        nc.sync.dma_start(k_win[0][:], k_rows[:, 0, :])
-        nc.sync.dma_start(k_win[1][:], k_rows[:, 1, :])
-        nc.sync.dma_start(k_win[2][:], k_rows[:, 2, :])
-        nc.sync.dma_start(k_win[3][:], k_rows[:, 3, :])
+        for t in range(4):
+            if t == 2:
+                nc.sync.dma_start(c_win[1][:], c_rows[:, 2, :])
+                nc.sync.dma_start(w_win[1][:], w_rows[:, 2, :])
+            nc.sync.dma_start(k_win[t][:], k_rows[:, t, :])
         nc.sync.dma_start(q_raw[:], qT[0].rearrange("(p t) n -> p t n", t=4))
         nc.vector.memset(ls_rows[:], 0.0)
         nc.scalar.dma_start(ls_rows[0:2, :], ls[0, 0, :].rearrange("(h p) -> h p", p=P))
@@ -57,119 +57,94 @@ def tile_attend_plw_rope_f_topk_kernel(tc, qT, kT, cT, wT, ls, offs, offs2, out_
         ident = sb.tile([P, P], F32, name="ident")
         make_identity(nc, ident[:])
 
-        prod_even = sb.tile([P, 4, N], F32, name="prod_even")
-        prod_odd = sb.tile([P, 4, N], F32, name="prod_odd")
         trig = [sb.tile([P, 3, N], F32, name="trig%d" % j) for j in range(2)]
 
-        trig_ps = [[], []]
-
-        def product(t, kg, dst, rows):
-            j = t // 2
-            parts = [(nc.vector, b, trig_ps[j][b][:, rows, :]) for b in range(3)]
-            parts.insert(2, (nc.gpsimd, 3, trig[j][:, rows, 3 * P : 4 * P]))
-            for engine, b, factors in parts:
-                cols = slice(b * P, (b + 1) * P)
-                keys = kg[b // 2][:, (b % 2) * P : (b % 2 + 1) * P]
-                engine.tensor_tensor(dst[:, 2 * j : 2 * j + 2, cols], keys.unsqueeze(1).to_broadcast([P, 2, P]), factors, MULT)
-
-        chunks = [slice(0, 128), slice(128, 320), slice(320, 512)]
-        words = [sb.tile([P, 2, c.stop - c.start], F32, name="words%d" % c.start) for c in chunks]
-        halves = [slice(0, HALF), slice(HALF, N)]
-        last = slice(3 * P, 4 * P)
-        minus_sines = []
-        for j in (0, 1):
-            trig_ps[j].extend(ps.tile([P, 3, P], F32, name="trig_ps%d%d" % (j, b), tag="bank%d" % (3 * j + b)) for b in range(3))
+        def factors(j):
             for row, win in ((1, c_win[j]), (2, w_win[j])):
-                nc.vector.tensor_copy(trig[j][:, row, :], win[:].indirect(pos[:]))
-                by_slot_ps = ps.tile([P, 3, P], F32, name="by_slot_ps%d%d" % (j, row), tag="bank%d" % (5 + row))
-                for b in range(3):
-                    nc.tensor.transpose(by_slot_ps[:, b, :], trig[j][:, row, b * P : (b + 1) * P], ident[:])
-                for dst_row in ((1,) if row == 1 else (2, 0)):
-                    by_slot = sb.tile([P, 3, P], F32, name="by_slot%d%d" % (j, dst_row))
-                    if dst_row == 0:
-                        nc.scalar.mul(by_slot[:], by_slot_ps[:], -1.0)
-                    else:
-                        nc.scalar.copy(by_slot[:], by_slot_ps[:])
-                    if dst_row == 0:
-                        minus_sines.append(by_slot)
-                        continue
-                    for b in range(3):
-                        nc.tensor.transpose(trig_ps[j][b][:, dst_row, :], by_slot[:, b, :], ident[:])
-            nc.scalar.mul(trig[j][:, 0, last], trig[j][:, 2, last], -1.0)
+                if j == 0:
+                    nc.vector.tensor_copy(trig[j][:, row, :], win[:].indirect(pos[:]))
+                else:
+                    nc.scalar.activation(trig[j][:, row, :], win[:].indirect(pos[:]), COPY)
+            nc.scalar.mul(trig[j][:, 0, :], trig[j][:, 2, :], -1.0)
 
-        for j in range(2):
-            for t, dst, rows in ((2 * j, prod_even, slice(1, 3)), (2 * j + 1, prod_odd, slice(0, 2))):
-                kg = [sb.tile([P, HALF], F32, name="kg%d%d" % (t, h)) for h in range(2)]
-                for h, cols in enumerate(halves):
-                    nc.vector.tensor_copy(kg[h][:], k_win[t][:].indirect(tok[:, cols.start // 16 : cols.stop // 16]))
-                if t < 3:
-                    product(t, kg, dst, rows)
-                if t % 2 == 0:
-                    for b in range(3):
-                        nc.tensor.transpose(trig_ps[j][b][:, 0, :], minus_sines[j][:, b, :], ident[:])
-            if j == 0:
-                back = ps.tile([P, 4, P], F32, name="back", tag="bank0")
-                summed = [ps.tile([P, 2, 2, P], F32, name="summed%d" % a, tag="bank%d" % (6 + a)) for a in range(2)]
-                for o, src in enumerate((prod_even, prod_odd)):
-                    for a in range(2):
-                        for b in range(2):
-                            cols = slice((2 * a + b) * P, (2 * a + b + 1) * P)
-                            for e in range(2):
-                                first = o == 0 and b == 0 and e == 0
-                                final = o == 1 and b == 1 and e == 1
-                                nc.tensor.matmul(summed[a][:, b, e, :], src[:, e, cols], ident[:], start=first, stop=final, is_transpose=True)
-                for a in range(2):
-                    rounded = sb.tile([P, 2, 2 * P], BF16, name="rounded%d" % a)
-                    nc.scalar.copy(rounded[:].rearrange("s b (p e) -> s b p e", e=2), summed[a][:].rearrange("s b e p -> s b p e"))
-                    for b in range(2):
-                        nc.tensor.transpose(back[:, 2 * a + b, :], rounded[:, b, :].bitcast(F32), ident[:])
-                back_row = back[:].rearrange("p c s -> p (c s)")
-                for c, cols in enumerate(chunks):
-                    nc.scalar.copy(words[c][:, 0, :], back_row[:, cols])
+        factors(0)
 
-        ls_cols_ps = ps.tile([P, P], F32, name="ls_cols_ps", tag="bank1")
+        ls_cols_ps = ps.tile([P, P], F32, name="ls_cols_ps")
         nc.tensor.transpose(ls_cols_ps[:], ls_rows[:], ident[:])
         ls_cols = sb.tile([P, 2], F32, name="ls_cols")
         nc.scalar.copy(ls_cols[:], ls_cols_ps[:, 0:2])
-        ls_wide_ps = ps.tile([P, 2, P], F32, name="ls_wide_ps", tag="bank2")
+        ls_wide_ps = ps.tile([P, 2, P], F32, name="ls_wide_ps")
         for h in range(2):
             nc.tensor.transpose(ls_wide_ps[:, h, :], ls_cols[:, h : h + 1].to_broadcast([P, P]), ident[:])
         ls_wide = sb.tile([P, NQ], F32, name="ls_wide")
         nc.scalar.copy(ls_wide[:], ls_wide_ps[:].rearrange("p h q -> p (h q)"))
+
+        words = [sb.tile([P, 2, P], F32, name="words%d" % r) for r in range(4)]
+
+        def products(t):
+            rows = slice(1, 3) if t % 2 == 0 else slice(0, 2)
+            prod = sb.tile([P, 4, P, 2], F32, name="prod%d" % t, tag="prod%d" % t)
+            keys = []
+            for b in range(4):
+                tag = ("kg00", "kg03", "prod0", "kg23")[t] if b == 0 else "kg%d%d" % (t, b)
+                kg = sb.tile([P, P], F32, name="kg%d%d" % (t, b), tag=tag)
+                listed = k_win[t][:].indirect(tok[:, 8 * b : 8 * (b + 1)])
+                if b == 0:
+                    nc.vector.tensor_copy(kg[:], listed)
+                else:
+                    nc.scalar.activation(kg[:], listed, COPY)
+                keys.append(kg)
+            for b in range(4):
+                nc.vector.tensor_tensor(
+                    prod[:, :, 32 * b : 32 * (b + 1), :].rearrange("p r s e -> p s r e"),
+                    keys[b][:].rearrange("p (s r) -> p s r", r=4).unsqueeze(3).to_broadcast([P, 32, 4, 2]),
+                    trig[t // 2][:, rows, b * P : (b + 1) * P].rearrange("p e (s r) -> p s r e", r=4),
+                    MULT,
+                )
+            return prod
+
+        def pair_sum(j, even, odd, r, cols):
+            nc.vector.tensor_tensor(
+                words[r][:, j, cols].bitcast(BF16),
+                even[:, r, cols, :].rearrange("p s e -> p (s e)"),
+                odd[:, r, cols, :].rearrange("p s e -> p (s e)"),
+                ADD,
+            )
+
+        first = [products(0), products(1)]
+        for r in range(4):
+            pair_sum(0, first[0], first[1], r, slice(0, P))
+        factors(1)
+        second = [products(2), products(3)]
 
         q_bf = sb.tile([P, NQ * 4], BF16, name="q_bf", align_bytes=64)
         q_codes = sb.tile([P, NQ], U32, name="q_codes", align_bytes=64)
         q_scales = sb.tile([P, NQ], U8, name="q_scales", align_bytes=64)
         nc.scalar.copy(q_bf[:].rearrange("p (c i t) -> p c t i", i=4, t=4), q_raw[:].rearrange("p t (c i) -> p c t i", i=4))
 
-        product(3, kg, prod_odd, slice(0, 2))
-        u_bf = sb.tile([P, 4, P * 4], BF16, name="u_bf", tag="q_then_u", align_bytes=64)
-        u_words = u_bf[:].bitcast(F32).rearrange("p r (s u) -> p s r u", u=2)
-        for c, cols in enumerate(chunks):
-            nc.vector.tensor_tensor(
-                words[c][:, 1, :].bitcast(BF16).rearrange("p (c i e) -> p c e i", i=4, e=2),
-                prod_even[:, 2:4, cols].rearrange("p e (c i) -> p c e i", i=4),
-                prod_odd[:, 2:4, cols].rearrange("p e (c i) -> p c e i", i=4),
-                ADD,
-            )
+        for cols in (slice(0, P // 2), slice(P // 2, P)):
+            for r in range(4):
+                pair_sum(1, second[0], second[1], r, cols)
 
-        def quantize_queries(h):
+        u_bf = sb.tile([P, 4, P * 4], BF16, name="u_bf", tag="q_then_u", align_bytes=64)
+
+        def weave(r):
+            dst = u_bf[:, r, :].bitcast(F32).rearrange("p (c i u) -> p c u i", i=2, u=2)
+            src = words[r][:].rearrange("p u (c i) -> p c u i", i=2)
+            if r == 0:
+                nc.vector.tensor_copy(dst, src)
+            else:
+                nc.scalar.copy(dst, src)
+
+        for r in range(4):
+            weave(r)
+        for h in range(2):
             qs = slice(h * P, (h + 1) * P)
             nc.vector.quantize_mx(out=q_codes[:, qs].bitcast(FP8X4), scales=q_scales[:, qs], in_=q_bf[:, h * 4 * P : (h + 1) * 4 * P])
 
-        quantize_queries(0)
-        for c, cols in enumerate(chunks):
-            dst = u_words[:, cols.start // 4 : cols.stop // 4]
-            src = words[c][:].rearrange("p u (s r) -> p s r u", r=4)
-            if c < 2:
-                nc.scalar.copy(dst, src)
-            else:
-                nc.vector.tensor_copy(dst, src)
-        quantize_queries(1)
-
         u_codes = [sb.tile([P, P], U32, name="u_codes%d" % r, align_bytes=64) for r in range(4)]
         u_scales = [sb.tile([P, P], U8, name="u_scales%d" % r, align_bytes=64) for r in range(4)]
-        score = [ps.tile([P, NQ], F32, name="score%d" % r, tag="bank%d" % (0, 1, 2, 7)[r]) for r in range(4)]
+        score = [ps.tile([P, NQ], F32, name="score%d" % r) for r in range(4)]
         for r in range(4):
             nc.vector.quantize_mx(out=u_codes[r][:].bitcast(FP8X4), scales=u_scales[r][:], in_=u_bf[:, r, :])
             nc.tensor.matmul_mx(

@@ -41,6 +41,8 @@ def tile_attend_plw_rope_f_topk_kernel(tc, qT, kT, cT, wT, ls, offs, offs2, out_
         q_raw = sb.tile([P, 4, NQ], F32, name="q_raw", tag="q_then_u", align_bytes=64)
         ls_rows = sb.tile([P, P], F32, name="ls_rows")
 
+        nc.gpsimd.memset(ls_rows[:], 0.0)
+        nc.scalar.dma_start(ls_rows[0:2, :], ls[0, 0, :].rearrange("(h p) -> h p", p=P))
         nc.sync.dma_start(c_win[0][:], c_rows[:, 0, :])
         nc.sync.dma_start(pos[:], offs2)
         nc.sync.dma_start(w_win[0][:], w_rows[:, 0, :])
@@ -51,11 +53,19 @@ def tile_attend_plw_rope_f_topk_kernel(tc, qT, kT, cT, wT, ls, offs, offs2, out_
                 nc.sync.dma_start(w_win[1][:], w_rows[:, 2, :])
             nc.sync.dma_start(k_win[t][:], k_rows[:, t, :])
         nc.sync.dma_start(q_raw[:], qT[0].rearrange("(p t) n -> p t n", t=4))
-        nc.vector.memset(ls_rows[:], 0.0)
-        nc.scalar.dma_start(ls_rows[0:2, :], ls[0, 0, :].rearrange("(h p) -> h p", p=P))
 
         ident = sb.tile([P, P], F32, name="ident")
         make_identity(nc, ident[:])
+
+        ls_cols_ps = ps.tile([P, P], F32, name="ls_cols_ps", tag="bank7")
+        nc.tensor.transpose(ls_cols_ps[:], ls_rows[:], ident[:])
+        ls_cols = sb.tile([P, 2], F32, name="ls_cols")
+        nc.scalar.copy(ls_cols[:], ls_cols_ps[:, 0:2])
+        ls_wide_ps = ps.tile([P, 2, P], F32, name="ls_wide_ps", tag="bank6")
+        for h in range(2):
+            nc.tensor.transpose(ls_wide_ps[:, h, :], ls_cols[:, h : h + 1].to_broadcast([P, P]), ident[:])
+        ls_wide = sb.tile([P, NQ], F32, name="ls_wide")
+        nc.scalar.copy(ls_wide[:], ls_wide_ps[:].rearrange("p h q -> p (h q)"))
 
         trig = [sb.tile([P, 3, N], F32, name="trig%d" % j) for j in range(2)]
 
@@ -67,53 +77,47 @@ def tile_attend_plw_rope_f_topk_kernel(tc, qT, kT, cT, wT, ls, offs, offs2, out_
                     nc.scalar.activation(trig[j][:, row, :], win[:].indirect(pos[:]), COPY)
             nc.scalar.mul(trig[j][:, 0, :], trig[j][:, 2, :], -1.0)
 
-        factors(0)
-
-        ls_cols_ps = ps.tile([P, P], F32, name="ls_cols_ps")
-        nc.tensor.transpose(ls_cols_ps[:], ls_rows[:], ident[:])
-        ls_cols = sb.tile([P, 2], F32, name="ls_cols")
-        nc.scalar.copy(ls_cols[:], ls_cols_ps[:, 0:2])
-        ls_wide_ps = ps.tile([P, 2, P], F32, name="ls_wide_ps")
-        for h in range(2):
-            nc.tensor.transpose(ls_wide_ps[:, h, :], ls_cols[:, h : h + 1].to_broadcast([P, P]), ident[:])
-        ls_wide = sb.tile([P, NQ], F32, name="ls_wide")
-        nc.scalar.copy(ls_wide[:], ls_wide_ps[:].rearrange("p h q -> p (h q)"))
-
-        words = [sb.tile([P, 2, P], F32, name="words%d" % r) for r in range(4)]
+        words = sb.tile([P, 4, 2, P], F32, name="words")
+        fused_tiles = []
 
         def products(t):
-            rows = slice(1, 3) if t % 2 == 0 else slice(0, 2)
+            rows = (1, 2) if t % 2 == 0 else (0, 1)
             prod = sb.tile([P, 4, P, 2], F32, name="prod%d" % t, tag="prod%d" % t)
-            keys = []
+            keys = {}
             for b in range(4):
-                tag = ("kg00", "kg03", "prod0", "kg23")[t] if b == 0 else "kg%d%d" % (t, b)
-                kg = sb.tile([P, P], F32, name="kg%d%d" % (t, b), tag=tag)
                 listed = k_win[t][:].indirect(tok[:, 8 * b : 8 * (b + 1)])
+                if t == 3 and b == 0:
+                    fused = sb.tile([P, 2, P], F32, name="fused", tag="kg23")
+                    fused_tiles.append(fused)
+                    for e in range(2):
+                        nc.vector.tensor_tensor(fused[:, e, :], listed, trig[1][:, rows[e], 0:P], MULT)
+                    continue
+                tag = ("kg00", "kg03", "prod0")[t] if b == 0 else "kg%d%d" % (t, b)
+                keys[b] = sb.tile([P, P], F32, name="kg%d%d" % (t, b), tag=tag)
                 if b == 0:
-                    nc.vector.tensor_copy(kg[:], listed)
+                    nc.vector.tensor_copy(keys[b][:], listed)
                 else:
-                    nc.scalar.activation(kg[:], listed, COPY)
-                keys.append(kg)
-            for b in range(4):
+                    nc.scalar.activation(keys[b][:], listed, COPY)
+            for b in keys:
                 nc.vector.tensor_tensor(
                     prod[:, :, 32 * b : 32 * (b + 1), :].rearrange("p r s e -> p s r e"),
                     keys[b][:].rearrange("p (s r) -> p s r", r=4).unsqueeze(3).to_broadcast([P, 32, 4, 2]),
-                    trig[t // 2][:, rows, b * P : (b + 1) * P].rearrange("p e (s r) -> p s r e", r=4),
+                    trig[t // 2][:, rows[0] : rows[1] + 1, b * P : (b + 1) * P].rearrange("p e (s r) -> p s r e", r=4),
                     MULT,
                 )
             return prod
 
-        def pair_sum(j, even, odd, r, cols):
+        def pair_sum(j, even, odd, rs, cols):
             nc.vector.tensor_tensor(
-                words[r][:, j, cols].bitcast(BF16),
-                even[:, r, cols, :].rearrange("p s e -> p (s e)"),
-                odd[:, r, cols, :].rearrange("p s e -> p (s e)"),
+                words[:, rs, j, cols].bitcast(BF16),
+                even[:, rs, cols, :].rearrange("p r s e -> p r (s e)"),
+                odd[:, rs, cols, :].rearrange("p r s e -> p r (s e)"),
                 ADD,
             )
 
+        factors(0)
         first = [products(0), products(1)]
-        for r in range(4):
-            pair_sum(0, first[0], first[1], r, slice(0, P))
+        pair_sum(0, first[0], first[1], slice(0, 4), slice(0, P))
         factors(1)
         second = [products(2), products(3)]
 
@@ -122,35 +126,40 @@ def tile_attend_plw_rope_f_topk_kernel(tc, qT, kT, cT, wT, ls, offs, offs2, out_
         q_scales = sb.tile([P, NQ], U8, name="q_scales", align_bytes=64)
         nc.scalar.copy(q_bf[:].rearrange("p (c i t) -> p c t i", i=4, t=4), q_raw[:].rearrange("p t (c i) -> p c t i", i=4))
 
-        for cols in (slice(0, P // 2), slice(P // 2, P)):
-            for r in range(4):
-                pair_sum(1, second[0], second[1], r, cols)
+        nc.vector.tensor_tensor(
+            words[:, :, 1, 0:32].bitcast(BF16).rearrange("p r (s e) -> p s r e", e=2),
+            second[0][:, :, 0:32, :].rearrange("p r s e -> p s r e"),
+            fused_tiles[0][:].rearrange("p e (s r) -> p s r e", r=4),
+            ADD,
+        )
+        for r in range(4):
+            pair_sum(1, second[0], second[1], slice(r, r + 1), slice(32, P))
 
-        u_bf = sb.tile([P, 4, P * 4], BF16, name="u_bf", tag="q_then_u", align_bytes=64)
+        u_bf = [sb.tile([P, P * 4], BF16, name="u_bf%d" % r, tag="q_then_u" if r == 0 else "u_bf%d" % r, align_bytes=64) for r in range(4)]
 
         def weave(r):
-            dst = u_bf[:, r, :].bitcast(F32).rearrange("p (c i u) -> p c u i", i=2, u=2)
-            src = words[r][:].rearrange("p u (c i) -> p c u i", i=2)
-            if r == 0:
+            dst = u_bf[r][:].bitcast(F32).rearrange("p (c i u) -> p c u i", i=2, u=2)
+            src = words[:, r].rearrange("p u (c i) -> p c u i", i=2)
+            if r == 3:
                 nc.vector.tensor_copy(dst, src)
             else:
                 nc.scalar.copy(dst, src)
 
-        for r in range(4):
+        for r in range(3):
             weave(r)
-        for h in range(2):
-            qs = slice(h * P, (h + 1) * P)
-            nc.vector.quantize_mx(out=q_codes[:, qs].bitcast(FP8X4), scales=q_scales[:, qs], in_=q_bf[:, h * 4 * P : (h + 1) * 4 * P])
+        nc.vector.quantize_mx(out=q_codes[:].bitcast(FP8X4), scales=q_scales[:], in_=q_bf[:])
 
         u_codes = [sb.tile([P, P], U32, name="u_codes%d" % r, align_bytes=64) for r in range(4)]
         u_scales = [sb.tile([P, P], U8, name="u_scales%d" % r, align_bytes=64) for r in range(4)]
-        score = [ps.tile([P, NQ], F32, name="score%d" % r) for r in range(4)]
+        score = [ps.tile([P, NQ], F32, name="score%d" % r, tag="bank%d" % (0, 1, 6, 7)[r]) for r in range(4)]
         for r in range(4):
-            nc.vector.quantize_mx(out=u_codes[r][:].bitcast(FP8X4), scales=u_scales[r][:], in_=u_bf[:, r, :])
+            nc.vector.quantize_mx(out=u_codes[r][:].bitcast(FP8X4), scales=u_scales[r][:], in_=u_bf[r][:])
             nc.tensor.matmul_mx(
                 out=score[r][:], lhsT=u_codes[r][:].bitcast(FP8X4), lhsT_scale=u_scales[r][:],
                 rhs=q_codes[:].bitcast(FP8X4), rhs_scale=q_scales[:], start=True, stop=True,
             )
+            if r == 0:
+                weave(3)
 
         y = sb.tile([P, 4, NQ], F32, name="y")
         out_rows = out_0.rearrange("(p r) q -> p r q", r=4)

@@ -78,31 +78,27 @@ def tile_attend_plw_rope_f_topk_kernel(tc, qT, kT, cT, wT, ls, offs, offs2, out_
             nc.scalar.mul(trig[j][:, 0, :], trig[j][:, 2, :], -1.0)
 
         words = sb.tile([P, 4, 2, P], F32, name="words")
-        fused_tiles = []
+        blocks = [slice(0, 64), slice(64, 192), slice(192, 352), slice(352, 512)]
 
         def products(t):
-            rows = (1, 2) if t % 2 == 0 else (0, 1)
+            rows = slice(1, 3) if t % 2 == 0 else slice(0, 2)
             prod = sb.tile([P, 4, P, 2], F32, name="prod%d" % t, tag="prod%d" % t)
-            keys = {}
-            for b in range(4):
-                listed = k_win[t][:].indirect(tok[:, 8 * b : 8 * (b + 1)])
-                if t == 3 and b == 0:
-                    fused = sb.tile([P, 2, P], F32, name="fused", tag="kg23")
-                    fused_tiles.append(fused)
-                    for e in range(2):
-                        nc.vector.tensor_tensor(fused[:, e, :], listed, trig[1][:, rows[e], 0:P], MULT)
-                    continue
-                tag = ("kg00", "kg03", "prod0")[t] if b == 0 else "kg%d%d" % (t, b)
-                keys[b] = sb.tile([P, P], F32, name="kg%d%d" % (t, b), tag=tag)
-                if b == 0:
-                    nc.vector.tensor_copy(keys[b][:], listed)
+            keys = []
+            for b, slots in enumerate(blocks):
+                tag = ("kg01", "kg03", "prod0", "kg23")[t] if b == 1 else "kg%d%d" % (t, b)
+                kg = sb.tile([P, slots.stop - slots.start], F32, name="kg%d%d" % (t, b), tag=tag)
+                listed = k_win[t][:].indirect(tok[:, slots.start // 16 : slots.stop // 16])
+                if b == 1:
+                    nc.vector.tensor_copy(kg[:], listed)
                 else:
-                    nc.scalar.activation(keys[b][:], listed, COPY)
-            for b in keys:
+                    nc.scalar.activation(kg[:], listed, COPY)
+                keys.append(kg)
+            for kg, slots in zip(keys, blocks):
+                rows_of_quarter = slice(slots.start // 4, slots.stop // 4)
                 nc.vector.tensor_tensor(
-                    prod[:, :, 32 * b : 32 * (b + 1), :].rearrange("p r s e -> p s r e"),
-                    keys[b][:].rearrange("p (s r) -> p s r", r=4).unsqueeze(3).to_broadcast([P, 32, 4, 2]),
-                    trig[t // 2][:, rows[0] : rows[1] + 1, b * P : (b + 1) * P].rearrange("p e (s r) -> p s r e", r=4),
+                    prod[:, :, rows_of_quarter, :].rearrange("p r s e -> p s r e"),
+                    kg[:].rearrange("p (s r) -> p s r", r=4).unsqueeze(3).to_broadcast([P, (slots.stop - slots.start) // 4, 4, 2]),
+                    trig[t // 2][:, rows, slots].rearrange("p e (s r) -> p s r e", r=4),
                     MULT,
                 )
             return prod
@@ -126,49 +122,63 @@ def tile_attend_plw_rope_f_topk_kernel(tc, qT, kT, cT, wT, ls, offs, offs2, out_
         q_scales = sb.tile([P, NQ], U8, name="q_scales", align_bytes=64)
         nc.scalar.copy(q_bf[:].rearrange("p (c i t) -> p c t i", i=4, t=4), q_raw[:].rearrange("p t (c i) -> p c t i", i=4))
 
-        nc.vector.tensor_tensor(
-            words[:, :, 1, 0:32].bitcast(BF16).rearrange("p r (s e) -> p s r e", e=2),
-            second[0][:, :, 0:32, :].rearrange("p r s e -> p s r e"),
-            fused_tiles[0][:].rearrange("p e (s r) -> p s r e", r=4),
-            ADD,
-        )
+        pair_sum(1, second[0], second[1], slice(0, 4), slice(0, 32))
         for r in range(4):
             pair_sum(1, second[0], second[1], slice(r, r + 1), slice(32, P))
 
         u_bf = [sb.tile([P, P * 4], BF16, name="u_bf%d" % r, tag="q_then_u" if r == 0 else "u_bf%d" % r, align_bytes=64) for r in range(4)]
 
-        def weave(r):
-            dst = u_bf[r][:].bitcast(F32).rearrange("p (c i u) -> p c u i", i=2, u=2)
-            src = words[:, r].rearrange("p u (c i) -> p c u i", i=2)
-            if r == 3:
-                nc.vector.tensor_copy(dst, src)
-            else:
-                nc.scalar.copy(dst, src)
+        def weave(copy, r):
+            copy(
+                u_bf[r][:].bitcast(F32).rearrange("p (c i u) -> p c u i", i=2, u=2),
+                words[:, r].rearrange("p u (c i) -> p c u i", i=2),
+            )
 
         for r in range(3):
-            weave(r)
-        nc.vector.quantize_mx(out=q_codes[:].bitcast(FP8X4), scales=q_scales[:], in_=q_bf[:])
+            weave(nc.scalar.copy, r)
 
+        halves = [slice(0, P), slice(P, NQ)]
         u_codes = [sb.tile([P, P], U32, name="u_codes%d" % r, align_bytes=64) for r in range(4)]
         u_scales = [sb.tile([P, P], U8, name="u_scales%d" % r, align_bytes=64) for r in range(4)]
-        score = [ps.tile([P, NQ], F32, name="score%d" % r, tag="bank%d" % (0, 1, 6, 7)[r]) for r in range(4)]
+        early = [ps.tile([P, NQ], F32, name="early%d" % r) for r in range(2)]
+        late = [ps.tile([P, 2, P], F32, name="late%d" % h) for h in range(2)]
+
+        def quantize_queries(h):
+            qs = halves[h]
+            nc.vector.quantize_mx(out=q_codes[:, qs].bitcast(FP8X4), scales=q_scales[:, qs], in_=q_bf[:, 4 * qs.start : 4 * qs.stop])
+
+        def scores(out, r, qs):
+            nc.tensor.matmul_mx(
+                out=out, lhsT=u_codes[r][:].bitcast(FP8X4), lhsT_scale=u_scales[r][:],
+                rhs=q_codes[:, qs].bitcast(FP8X4), rhs_scale=q_scales[:, qs], start=True, stop=True,
+            )
+
+        quantize_queries(0)
         for r in range(4):
             nc.vector.quantize_mx(out=u_codes[r][:].bitcast(FP8X4), scales=u_scales[r][:], in_=u_bf[r][:])
-            nc.tensor.matmul_mx(
-                out=score[r][:], lhsT=u_codes[r][:].bitcast(FP8X4), lhsT_scale=u_scales[r][:],
-                rhs=q_codes[:].bitcast(FP8X4), rhs_scale=q_scales[:], start=True, stop=True,
-            )
             if r == 0:
-                weave(3)
+                scores(early[0][:, halves[0]], 0, halves[0])
+                quantize_queries(1)
+                scores(early[0][:, halves[1]], 0, halves[1])
+                weave(nc.vector.tensor_copy, 3)
+            elif r == 1:
+                scores(early[1][:], 1, slice(0, NQ))
+            else:
+                for h in range(2):
+                    scores(late[h][:, r - 2, :], r, halves[h])
 
         y = sb.tile([P, 4, NQ], F32, name="y")
         out_rows = out_0.rearrange("(p r) q -> p r q", r=4)
-        for r in range(4):
+        for r in range(2):
             shifted = sb.tile([P, NQ], F32, name="shifted%d" % r)
-            nc.vector.tensor_tensor(shifted[:], score[r][:], ls_wide[:], SUB)
+            nc.vector.tensor_tensor(shifted[:], early[r][:], ls_wide[:], SUB)
             nc.scalar.activation(y[:, r, :], shifted[:], EXP)
-            if r % 2 == 1:
-                nc.sync.dma_start(out_rows[:, r - 1 : r + 1, :], y[:, r - 1 : r + 1, :])
+        nc.sync.dma_start(out_rows[:, 0:2, :], y[:, 0:2, :])
+        for h in range(2):
+            shifted = sb.tile([P, 2, P], F32, name="shifted_late%d" % h)
+            nc.vector.tensor_tensor(shifted[:], late[h][:], ls_wide[:, halves[h]].unsqueeze(1).to_broadcast([P, 2, P]), SUB)
+            nc.scalar.activation(y[:, 2:4, halves[h]], shifted[:], EXP)
+        nc.sync.dma_start(out_rows[:, 2:4, :], y[:, 2:4, :])
 
         y_bf = [sb.tile([P, P * 4], BF16, name="y_bf%d" % h, align_bytes=64) for h in range(2)]
         y_codes = sb.tile([P, NQ], U32, name="y_codes", align_bytes=64)

@@ -21,7 +21,12 @@ EXP = mybir.ActivationFunctionType.Exp
 COPY = mybir.ActivationFunctionType.Copy
 
 P = 128
-HALF = N // 2
+
+SLOT_BLOCKS = [slice(0, 64), slice(64, 192), slice(192, 352), slice(352, 512)]
+VECTOR_BLOCK = 1
+EARLY_ROWS = 32
+QUERY_HALVES = [slice(0, P), slice(P, NQ)]
+QUERY_PIECES = [slice(0, 128), slice(128, 192), slice(192, 256)]
 
 
 def tile_attend_plw_rope_f_topk_kernel(tc, qT, kT, cT, wT, ls, offs, offs2, out_0, out_1, out_2):
@@ -47,11 +52,12 @@ def tile_attend_plw_rope_f_topk_kernel(tc, qT, kT, cT, wT, ls, offs, offs2, out_
         nc.sync.dma_start(pos[:], offs2)
         nc.sync.dma_start(w_win[0][:], w_rows[:, 0, :])
         nc.sync.dma_start(tok[:], offs)
-        for t in range(4):
-            if t == 2:
-                nc.sync.dma_start(c_win[1][:], c_rows[:, 2, :])
-                nc.sync.dma_start(w_win[1][:], w_rows[:, 2, :])
-            nc.sync.dma_start(k_win[t][:], k_rows[:, t, :])
+        nc.sync.dma_start(k_win[0][:], k_rows[:, 0, :])
+        nc.sync.dma_start(k_win[1][:], k_rows[:, 1, :])
+        nc.sync.dma_start(c_win[1][:], c_rows[:, 2, :])
+        nc.sync.dma_start(w_win[1][:], w_rows[:, 2, :])
+        nc.sync.dma_start(k_win[2][:], k_rows[:, 2, :])
+        nc.sync.dma_start(k_win[3][:], k_rows[:, 3, :])
         nc.sync.dma_start(q_raw[:], qT[0].rearrange("(p t) n -> p t n", t=4))
 
         ident = sb.tile([P, P], F32, name="ident")
@@ -78,36 +84,37 @@ def tile_attend_plw_rope_f_topk_kernel(tc, qT, kT, cT, wT, ls, offs, offs2, out_
             nc.scalar.mul(trig[j][:, 0, :], trig[j][:, 2, :], -1.0)
 
         words = sb.tile([P, 4, 2, P], F32, name="words")
-        blocks = [slice(0, 64), slice(64, 192), slice(192, 352), slice(352, 512)]
+
+        vector_block_tags = ("kg01", "kg03", "prod0", "kg23")
 
         def products(t):
             rows = slice(1, 3) if t % 2 == 0 else slice(0, 2)
             prod = sb.tile([P, 4, P, 2], F32, name="prod%d" % t, tag="prod%d" % t)
             keys = []
-            for b, slots in enumerate(blocks):
-                tag = ("kg01", "kg03", "prod0", "kg23")[t] if b == 1 else "kg%d%d" % (t, b)
+            for b, slots in enumerate(SLOT_BLOCKS):
+                tag = vector_block_tags[t] if b == VECTOR_BLOCK else "kg%d%d" % (t, b)
                 kg = sb.tile([P, slots.stop - slots.start], F32, name="kg%d%d" % (t, b), tag=tag)
                 listed = k_win[t][:].indirect(tok[:, slots.start // 16 : slots.stop // 16])
-                if b == 1:
+                if b == VECTOR_BLOCK:
                     nc.vector.tensor_copy(kg[:], listed)
                 else:
                     nc.scalar.activation(kg[:], listed, COPY)
                 keys.append(kg)
-            for kg, slots in zip(keys, blocks):
-                rows_of_quarter = slice(slots.start // 4, slots.stop // 4)
+            for kg, slots in zip(keys, SLOT_BLOCKS):
+                s_rows = slice(slots.start // 4, slots.stop // 4)
                 nc.vector.tensor_tensor(
-                    prod[:, :, rows_of_quarter, :].rearrange("p r s e -> p s r e"),
-                    kg[:].rearrange("p (s r) -> p s r", r=4).unsqueeze(3).to_broadcast([P, (slots.stop - slots.start) // 4, 4, 2]),
+                    prod[:, :, s_rows, :].rearrange("p r s e -> p s r e"),
+                    kg[:].rearrange("p (s r) -> p s r", r=4).unsqueeze(3).to_broadcast([P, s_rows.stop - s_rows.start, 4, 2]),
                     trig[t // 2][:, rows, slots].rearrange("p e (s r) -> p s r e", r=4),
                     MULT,
                 )
             return prod
 
-        def pair_sum(j, even, odd, rs, cols):
+        def pair_sum(j, even, odd, quarters, s_rows):
             nc.vector.tensor_tensor(
-                words[:, rs, j, cols].bitcast(BF16),
-                even[:, rs, cols, :].rearrange("p r s e -> p r (s e)"),
-                odd[:, rs, cols, :].rearrange("p r s e -> p r (s e)"),
+                words[:, quarters, j, s_rows].bitcast(BF16),
+                even[:, quarters, s_rows, :].rearrange("p r s e -> p r (s e)"),
+                odd[:, quarters, s_rows, :].rearrange("p r s e -> p r (s e)"),
                 ADD,
             )
 
@@ -122,30 +129,31 @@ def tile_attend_plw_rope_f_topk_kernel(tc, qT, kT, cT, wT, ls, offs, offs2, out_
         q_scales = sb.tile([P, NQ], U8, name="q_scales", align_bytes=64)
         nc.scalar.copy(q_bf[:].rearrange("p (c i t) -> p c t i", i=4, t=4), q_raw[:].rearrange("p t (c i) -> p c t i", i=4))
 
-        pair_sum(1, second[0], second[1], slice(0, 4), slice(0, 32))
+        pair_sum(1, second[0], second[1], slice(0, 4), slice(0, EARLY_ROWS))
         for r in range(4):
-            pair_sum(1, second[0], second[1], slice(r, r + 1), slice(32, P))
+            pair_sum(1, second[0], second[1], slice(r, r + 1), slice(EARLY_ROWS, P))
 
         u_bf = [sb.tile([P, P * 4], BF16, name="u_bf%d" % r, tag="q_then_u" if r == 0 else "u_bf%d" % r, align_bytes=64) for r in range(4)]
 
-        def weave(copy, r):
+        def interleave(copy, r):
             copy(
-                u_bf[r][:].bitcast(F32).rearrange("p (c i u) -> p c u i", i=2, u=2),
-                words[:, r].rearrange("p u (c i) -> p c u i", i=2),
+                u_bf[r][:].bitcast(F32).rearrange("p (c i j) -> p c j i", i=2, j=2),
+                words[:, r].rearrange("p j (c i) -> p c j i", i=2),
             )
 
         for r in range(3):
-            weave(nc.scalar.copy, r)
+            interleave(nc.scalar.copy, r)
 
-        halves = [slice(0, P), slice(P, NQ)]
         u_codes = [sb.tile([P, P], U32, name="u_codes%d" % r, align_bytes=64) for r in range(4)]
         u_scales = [sb.tile([P, P], U8, name="u_scales%d" % r, align_bytes=64) for r in range(4)]
         early = [ps.tile([P, NQ], F32, name="early%d" % r) for r in range(2)]
         late = [ps.tile([P, 2, P], F32, name="late%d" % h) for h in range(2)]
 
-        def quantize_queries(h):
-            qs = halves[h]
+        def quantize_queries(qs):
             nc.vector.quantize_mx(out=q_codes[:, qs].bitcast(FP8X4), scales=q_scales[:, qs], in_=q_bf[:, 4 * qs.start : 4 * qs.stop])
+
+        def quantize_keys(r):
+            nc.vector.quantize_mx(out=u_codes[r][:].bitcast(FP8X4), scales=u_scales[r][:], in_=u_bf[r][:])
 
         def scores(out, r, qs):
             nc.tensor.matmul_mx(
@@ -153,19 +161,19 @@ def tile_attend_plw_rope_f_topk_kernel(tc, qT, kT, cT, wT, ls, offs, offs2, out_
                 rhs=q_codes[:, qs].bitcast(FP8X4), rhs_scale=q_scales[:, qs], start=True, stop=True,
             )
 
-        quantize_queries(0)
-        for r in range(4):
-            nc.vector.quantize_mx(out=u_codes[r][:].bitcast(FP8X4), scales=u_scales[r][:], in_=u_bf[r][:])
-            if r == 0:
-                scores(early[0][:, halves[0]], 0, halves[0])
-                quantize_queries(1)
-                scores(early[0][:, halves[1]], 0, halves[1])
-                weave(nc.vector.tensor_copy, 3)
-            elif r == 1:
-                scores(early[1][:], 1, slice(0, NQ))
-            else:
-                for h in range(2):
-                    scores(late[h][:, r - 2, :], r, halves[h])
+        quantize_queries(QUERY_HALVES[0])
+        quantize_keys(0)
+        scores(early[0][:, QUERY_HALVES[0]], 0, QUERY_HALVES[0])
+        quantize_queries(QUERY_HALVES[1])
+        scores(early[0][:, QUERY_HALVES[1]], 0, QUERY_HALVES[1])
+        interleave(nc.vector.tensor_copy, 3)
+        quantize_keys(1)
+        scores(early[1][:], 1, slice(0, NQ))
+        quantize_keys(2)
+        quantize_keys(3)
+        for h, qs in enumerate(QUERY_HALVES):
+            for r in (2, 3):
+                scores(late[h][:, r - 2, :], r, qs)
 
         y = sb.tile([P, 4, NQ], F32, name="y")
         out_rows = out_0.rearrange("(p r) q -> p r q", r=4)
@@ -174,22 +182,26 @@ def tile_attend_plw_rope_f_topk_kernel(tc, qT, kT, cT, wT, ls, offs, offs2, out_
             nc.vector.tensor_tensor(shifted[:], early[r][:], ls_wide[:], SUB)
             nc.scalar.activation(y[:, r, :], shifted[:], EXP)
         nc.sync.dma_start(out_rows[:, 0:2, :], y[:, 0:2, :])
-        for h in range(2):
-            shifted = sb.tile([P, 2, P], F32, name="shifted_late%d" % h)
-            nc.vector.tensor_tensor(shifted[:], late[h][:], ls_wide[:, halves[h]].unsqueeze(1).to_broadcast([P, 2, P]), SUB)
-            nc.scalar.activation(y[:, 2:4, halves[h]], shifted[:], EXP)
+        for qs in QUERY_PIECES:
+            width = qs.stop - qs.start
+            shifted = sb.tile([P, 2, width], F32, name="shifted_late%d" % qs.start)
+            bank = late[qs.start // P][:, :, qs.start % P : qs.start % P + width]
+            nc.vector.tensor_tensor(shifted[:], bank, ls_wide[:, qs].unsqueeze(1).to_broadcast([P, 2, width]), SUB)
+            nc.scalar.activation(y[:, 2:4, qs], shifted[:], EXP)
         nc.sync.dma_start(out_rows[:, 2:4, :], y[:, 2:4, :])
 
-        y_bf = [sb.tile([P, P * 4], BF16, name="y_bf%d" % h, align_bytes=64) for h in range(2)]
+        y_bf = [sb.tile([P, 4 * (qs.stop - qs.start)], BF16, name="y_bf%d" % qs.start, align_bytes=64) for qs in QUERY_PIECES]
         y_codes = sb.tile([P, NQ], U32, name="y_codes", align_bytes=64)
         y_scales = sb.tile([P, NQ], U8, name="y_scales", align_bytes=64)
-        for rs in (slice(0, 2), slice(2, 4)):
-            for h in range(2):
-                qs = slice(h * P, (h + 1) * P)
-                nc.vector.tensor_copy(y_bf[h][:].rearrange("p (c i r) -> p c r i", i=4, r=4)[:, :, rs], y[:, rs, qs].rearrange("p r (c i) -> p c r i", i=4))
-        for h in range(2):
-            qs = slice(h * P, (h + 1) * P)
-            nc.vector.quantize_mx(out=y_codes[:, qs].bitcast(FP8X4), scales=y_scales[:, qs], in_=y_bf[h][:])
+        for quarters in (slice(0, 2), slice(2, 4)):
+            for piece_bf, qs in zip(y_bf, QUERY_PIECES):
+                nc.vector.tensor_copy(
+                    piece_bf[:].rearrange("p (c i r) -> p c r i", i=4, r=4)[:, :, quarters],
+                    y[:, quarters, qs].rearrange("p r (c i) -> p c r i", i=4),
+                )
+        for piece_bf, qs in zip(y_bf, QUERY_PIECES):
+            nc.vector.quantize_mx(out=y_codes[:, qs].bitcast(FP8X4), scales=y_scales[:, qs], in_=piece_bf[:])
+
         nc.sync.dma_start(out_1[0].rearrange("p q x -> p (q x)").bitcast(I32), y_codes[:].bitcast(I32))
         for quad in range(4):
             queue = nc.scalar if quad % 2 == 0 else nc.sync

@@ -24,7 +24,7 @@ P = 128
 
 SLOT_BLOCKS = [slice(0, 64), slice(64, 192), slice(192, 352), slice(352, 512)]
 VECTOR_BLOCK = 1
-EARLY_ROWS = 32
+EARLY_ROWS = 88
 QUERY_HALVES = [slice(0, P), slice(P, NQ)]
 QUERY_PIECES = [slice(0, 128), slice(128, 192), slice(192, 256)]
 
@@ -33,6 +33,7 @@ def tile_attend_plw_rope_f_topk_kernel(tc, qT, kT, cT, wT, ls, offs, offs2, out_
     nc = tc.nc
     with ExitStack() as ctx:
         sb = ctx.enter_context(tc.tile_pool(name="sb", bufs=1))
+        shared = ctx.enter_context(tc.tile_pool(name="shared", bufs=1))
         ps = ctx.enter_context(tc.psum_pool(name="ps", bufs=1))
 
         tok = sb.tile([P, N // 16], U16, name="tok")
@@ -43,7 +44,7 @@ def tile_attend_plw_rope_f_topk_kernel(tc, qT, kT, cT, wT, ls, offs, offs2, out_
         k_win = [sb.tile([P, T], F32, name="k_win%d" % t) for t in range(4)]
         c_win = [sb.tile([P, NPOS], F32, name="c_win%d" % j) for j in range(2)]
         w_win = [sb.tile([P, NPOS], F32, name="w_win%d" % j) for j in range(2)]
-        q_raw = sb.tile([P, 4, NQ], F32, name="q_raw", tag="q_then_u", align_bytes=64)
+        q_raw = shared.tile([P, 4, NQ], F32, name="q_raw", offset=0, align_bytes=64)
         ls_rows = sb.tile([P, P], F32, name="ls_rows")
 
         nc.gpsimd.memset(ls_rows[:], 0.0)
@@ -83,7 +84,7 @@ def tile_attend_plw_rope_f_topk_kernel(tc, qT, kT, cT, wT, ls, offs, offs2, out_
                     nc.scalar.activation(trig[j][:, row, :], win[:].indirect(pos[:]), COPY)
             nc.scalar.mul(trig[j][:, 0, :], trig[j][:, 2, :], -1.0)
 
-        words = sb.tile([P, 4, 2, P], F32, name="words")
+        words = [sb.tile([P, 2, P], F32, name="words%d" % r) for r in range(4)]
 
         vector_block_tags = ("kg01", "kg03", "prod0", "kg23")
 
@@ -110,17 +111,18 @@ def tile_attend_plw_rope_f_topk_kernel(tc, qT, kT, cT, wT, ls, offs, offs2, out_
                 )
             return prod
 
-        def pair_sum(j, even, odd, quarters, s_rows):
+        def pair_sum(j, even, odd, r, s_rows):
             nc.vector.tensor_tensor(
-                words[:, quarters, j, s_rows].bitcast(BF16),
-                even[:, quarters, s_rows, :].rearrange("p r s e -> p r (s e)"),
-                odd[:, quarters, s_rows, :].rearrange("p r s e -> p r (s e)"),
+                words[r][:, j, s_rows].bitcast(BF16),
+                even[:, r, s_rows, :].rearrange("p s e -> p (s e)"),
+                odd[:, r, s_rows, :].rearrange("p s e -> p (s e)"),
                 ADD,
             )
 
         factors(0)
         first = [products(0), products(1)]
-        pair_sum(0, first[0], first[1], slice(0, 4), slice(0, P))
+        for r in range(4):
+            pair_sum(0, first[0], first[1], r, slice(0, P))
         factors(1)
         second = [products(2), products(3)]
 
@@ -129,19 +131,20 @@ def tile_attend_plw_rope_f_topk_kernel(tc, qT, kT, cT, wT, ls, offs, offs2, out_
         q_scales = sb.tile([P, NQ], U8, name="q_scales", align_bytes=64)
         nc.scalar.copy(q_bf[:].rearrange("p (c i t) -> p c t i", i=4, t=4), q_raw[:].rearrange("p t (c i) -> p c t i", i=4))
 
-        pair_sum(1, second[0], second[1], slice(0, 4), slice(0, EARLY_ROWS))
-        for r in range(4):
-            pair_sum(1, second[0], second[1], slice(r, r + 1), slice(EARLY_ROWS, P))
+        pair_sum(1, second[0], second[1], 0, slice(0, EARLY_ROWS))
+        pair_sum(1, second[0], second[1], 0, slice(EARLY_ROWS, P))
+        for r in range(1, 4):
+            pair_sum(1, second[0], second[1], r, slice(0, P))
 
-        u_bf = [sb.tile([P, P * 4], BF16, name="u_bf%d" % r, tag="q_then_u" if r == 0 else "u_bf%d" % r, align_bytes=64) for r in range(4)]
+        u_bf = [shared.tile([P, P * 4], BF16, name="u_bf%d" % r, offset=r * P * 4 * 2, align_bytes=64) for r in range(4)]
 
         def interleave(copy, r):
             copy(
                 u_bf[r][:].bitcast(F32).rearrange("p (c i j) -> p c j i", i=2, j=2),
-                words[:, r].rearrange("p j (c i) -> p c j i", i=2),
+                words[r][:].rearrange("p j (c i) -> p c j i", i=2),
             )
 
-        for r in range(3):
+        for r in range(4):
             interleave(nc.scalar.copy, r)
 
         u_codes = [sb.tile([P, P], U32, name="u_codes%d" % r, align_bytes=64) for r in range(4)]
@@ -161,12 +164,9 @@ def tile_attend_plw_rope_f_topk_kernel(tc, qT, kT, cT, wT, ls, offs, offs2, out_
                 rhs=q_codes[:, qs].bitcast(FP8X4), rhs_scale=q_scales[:, qs], start=True, stop=True,
             )
 
-        quantize_queries(QUERY_HALVES[0])
+        quantize_queries(slice(0, NQ))
         quantize_keys(0)
-        scores(early[0][:, QUERY_HALVES[0]], 0, QUERY_HALVES[0])
-        quantize_queries(QUERY_HALVES[1])
-        scores(early[0][:, QUERY_HALVES[1]], 0, QUERY_HALVES[1])
-        interleave(nc.vector.tensor_copy, 3)
+        scores(early[0][:], 0, slice(0, NQ))
         quantize_keys(1)
         scores(early[1][:], 1, slice(0, NQ))
         quantize_keys(2)
@@ -178,7 +178,7 @@ def tile_attend_plw_rope_f_topk_kernel(tc, qT, kT, cT, wT, ls, offs, offs2, out_
         y = sb.tile([P, 4, NQ], F32, name="y")
         out_rows = out_0.rearrange("(p r) q -> p r q", r=4)
         for r in range(2):
-            shifted = sb.tile([P, NQ], F32, name="shifted%d" % r)
+            shifted = shared.tile([P, NQ], F32, name="shifted%d" % r, offset=2560 + 1024 * r, align_bytes=64)
             nc.vector.tensor_tensor(shifted[:], early[r][:], ls_wide[:], SUB)
             nc.scalar.activation(y[:, r, :], shifted[:], EXP)
         nc.sync.dma_start(out_rows[:, 0:2, :], y[:, 0:2, :])
@@ -193,12 +193,11 @@ def tile_attend_plw_rope_f_topk_kernel(tc, qT, kT, cT, wT, ls, offs, offs2, out_
         y_bf = [sb.tile([P, 4 * (qs.stop - qs.start)], BF16, name="y_bf%d" % qs.start, align_bytes=64) for qs in QUERY_PIECES]
         y_codes = sb.tile([P, NQ], U32, name="y_codes", align_bytes=64)
         y_scales = sb.tile([P, NQ], U8, name="y_scales", align_bytes=64)
-        for quarters in (slice(0, 2), slice(2, 4)):
-            for piece_bf, qs in zip(y_bf, QUERY_PIECES):
-                nc.vector.tensor_copy(
-                    piece_bf[:].rearrange("p (c i r) -> p c r i", i=4, r=4)[:, :, quarters],
-                    y[:, quarters, qs].rearrange("p r (c i) -> p c r i", i=4),
-                )
+        for piece_bf, qs in zip(y_bf, QUERY_PIECES):
+            nc.vector.tensor_copy(
+                piece_bf[:].rearrange("p (c i r) -> p c r i", i=4, r=4),
+                y[:, :, qs].rearrange("p r (c i) -> p c r i", i=4),
+            )
         for piece_bf, qs in zip(y_bf, QUERY_PIECES):
             nc.vector.quantize_mx(out=y_codes[:, qs].bitcast(FP8X4), scales=y_scales[:, qs], in_=piece_bf[:])
 

@@ -193,11 +193,12 @@ def tile_attend_plw_rope_f_topk_kernel(tc, qT, kT, cT, wT, ls, offs, offs2, out_
         y_bf = [sb.tile([P, 4 * (qs.stop - qs.start)], BF16, name="y_bf%d" % qs.start, align_bytes=64) for qs in QUERY_PIECES]
         y_codes = sb.tile([P, NQ], U32, name="y_codes", align_bytes=64)
         y_scales = sb.tile([P, NQ], U8, name="y_scales", align_bytes=64)
-        for piece_bf, qs in zip(y_bf, QUERY_PIECES):
-            nc.vector.tensor_copy(
-                piece_bf[:].rearrange("p (c i r) -> p c r i", i=4, r=4),
-                y[:, :, qs].rearrange("p r (c i) -> p c r i", i=4),
-            )
+        for quarters in (slice(0, 2), slice(2, 4)):
+            for piece_bf, qs in zip(y_bf, QUERY_PIECES):
+                nc.vector.tensor_copy(
+                    piece_bf[:].rearrange("p (c i r) -> p c r i", i=4, r=4)[:, :, quarters],
+                    y[:, quarters, qs].rearrange("p r (c i) -> p c r i", i=4),
+                )
         for piece_bf, qs in zip(y_bf, QUERY_PIECES):
             nc.vector.quantize_mx(out=y_codes[:, qs].bitcast(FP8X4), scales=y_scales[:, qs], in_=piece_bf[:])
 

@@ -15,7 +15,6 @@ U16 = mybir.dt.uint16
 U8 = mybir.dt.uint8
 FP8X4 = mybir.dt.float8_e4m3fn_x4
 MULT = mybir.AluOpType.mult
-ADD = mybir.AluOpType.add
 SUB = mybir.AluOpType.subtract
 EXP = mybir.ActivationFunctionType.Exp
 COPY = mybir.ActivationFunctionType.Copy
@@ -26,7 +25,7 @@ SLOT_BLOCKS = [slice(0, 64), slice(64, 192), slice(192, 352), slice(352, 512)]
 VECTOR_BLOCK = 1
 EARLY_ROWS = 88
 QUERY_HALVES = [slice(0, P), slice(P, NQ)]
-QUERY_PIECES = [slice(0, 128), slice(128, 192), slice(192, 256)]
+QUERY_PIECES = [slice(q, q + 64) for q in range(0, NQ, 64)]
 
 
 def tile_attend_plw_rope_f_topk_kernel(tc, qT, kT, cT, wT, ls, offs, offs2, out_0, out_1, out_2):
@@ -44,7 +43,7 @@ def tile_attend_plw_rope_f_topk_kernel(tc, qT, kT, cT, wT, ls, offs, offs2, out_
         k_win = [sb.tile([P, T], F32, name="k_win%d" % t) for t in range(4)]
         c_win = [sb.tile([P, NPOS], F32, name="c_win%d" % j) for j in range(2)]
         w_win = [sb.tile([P, NPOS], F32, name="w_win%d" % j) for j in range(2)]
-        q_raw = shared.tile([P, 4, NQ], F32, name="q_raw", offset=0, align_bytes=64)
+        q_raw = sb.tile([P, 4, NQ], F32, name="q_raw")
         ls_rows = sb.tile([P, P], F32, name="ls_rows")
 
         nc.gpsimd.memset(ls_rows[:], 0.0)
@@ -77,19 +76,22 @@ def tile_attend_plw_rope_f_topk_kernel(tc, qT, kT, cT, wT, ls, offs, offs2, out_
         trig = [sb.tile([P, 3, N], F32, name="trig%d" % j) for j in range(2)]
 
         def factors(j):
-            for row, win in ((1, c_win[j]), (2, w_win[j])):
+            for row, win in ((0, c_win[j]), (1, w_win[j])):
                 if j == 0:
                     nc.vector.tensor_copy(trig[j][:, row, :], win[:].indirect(pos[:]))
                 else:
                     nc.scalar.activation(trig[j][:, row, :], win[:].indirect(pos[:]), COPY)
-            nc.scalar.mul(trig[j][:, 0, :], trig[j][:, 2, :], -1.0)
+                if row == 0 and j == 0:
+                    nc.scalar.mul(trig[j][:, 2, :], trig[j][:, 0, :], -1.0)
+                elif row == 0:
+                    nc.vector.tensor_scalar_mul(trig[j][:, 2, :], trig[j][:, 0, :], -1.0)
 
         words = [sb.tile([P, 2, P], F32, name="words%d" % r) for r in range(4)]
 
         vector_block_tags = ("kg01", "kg03", "prod0", "kg23")
 
         def products(t):
-            rows = slice(1, 3) if t % 2 == 0 else slice(0, 2)
+            rows = slice(0, 2) if t % 2 == 0 else slice(1, 3)
             prod = sb.tile([P, 4, P, 2], F32, name="prod%d" % t, tag="prod%d" % t)
             keys = []
             for b, slots in enumerate(SLOT_BLOCKS):
@@ -116,7 +118,7 @@ def tile_attend_plw_rope_f_topk_kernel(tc, qT, kT, cT, wT, ls, offs, offs2, out_
                 words[r][:, j, s_rows].bitcast(BF16),
                 even[:, r, s_rows, :].rearrange("p s e -> p (s e)"),
                 odd[:, r, s_rows, :].rearrange("p s e -> p (s e)"),
-                ADD,
+                SUB,
             )
 
         factors(0)
@@ -164,9 +166,11 @@ def tile_attend_plw_rope_f_topk_kernel(tc, qT, kT, cT, wT, ls, offs, offs2, out_
                 rhs=q_codes[:, qs].bitcast(FP8X4), rhs_scale=q_scales[:, qs], start=True, stop=True,
             )
 
-        quantize_queries(slice(0, NQ))
+        quantize_queries(QUERY_HALVES[0])
         quantize_keys(0)
-        scores(early[0][:], 0, slice(0, NQ))
+        scores(early[0][:, QUERY_HALVES[0]], 0, QUERY_HALVES[0])
+        quantize_queries(QUERY_HALVES[1])
+        scores(early[0][:, QUERY_HALVES[1]], 0, QUERY_HALVES[1])
         quantize_keys(1)
         scores(early[1][:], 1, slice(0, NQ))
         quantize_keys(2)
@@ -190,17 +194,22 @@ def tile_attend_plw_rope_f_topk_kernel(tc, qT, kT, cT, wT, ls, offs, offs2, out_
             nc.scalar.activation(y[:, 2:4, qs], shifted[:], EXP)
         nc.sync.dma_start(out_rows[:, 2:4, :], y[:, 2:4, :])
 
-        y_bf = [sb.tile([P, 4 * (qs.stop - qs.start)], BF16, name="y_bf%d" % qs.start, align_bytes=64) for qs in QUERY_PIECES]
+        y_bf = sb.tile([P, 4 * NQ], BF16, name="y_bf", align_bytes=64)
         y_codes = sb.tile([P, NQ], U32, name="y_codes", align_bytes=64)
         y_scales = sb.tile([P, NQ], U8, name="y_scales", align_bytes=64)
-        for quarters in (slice(0, 2), slice(2, 4)):
-            for piece_bf, qs in zip(y_bf, QUERY_PIECES):
-                nc.vector.tensor_copy(
-                    piece_bf[:].rearrange("p (c i r) -> p c r i", i=4, r=4)[:, :, quarters],
-                    y[:, quarters, qs].rearrange("p r (c i) -> p c r i", i=4),
-                )
-        for piece_bf, qs in zip(y_bf, QUERY_PIECES):
-            nc.vector.quantize_mx(out=y_codes[:, qs].bitcast(FP8X4), scales=y_scales[:, qs], in_=piece_bf[:])
+
+        def round_result(quarters, qs):
+            nc.vector.tensor_copy(
+                y_bf[:, 4 * qs.start : 4 * qs.stop].rearrange("p (c i r) -> p c r i", i=4, r=4)[:, :, quarters],
+                y[:, quarters, qs].rearrange("p r (c i) -> p c r i", i=4),
+            )
+
+        for qs in QUERY_HALVES:
+            round_result(slice(0, 2), qs)
+        for qs in QUERY_PIECES:
+            round_result(slice(2, 4), qs)
+        for qs in QUERY_PIECES:
+            nc.vector.quantize_mx(out=y_codes[:, qs].bitcast(FP8X4), scales=y_scales[:, qs], in_=y_bf[:, 4 * qs.start : 4 * qs.stop])
 
         nc.sync.dma_start(out_1[0].rearrange("p q x -> p (q x)").bitcast(I32), y_codes[:].bitcast(I32))
         for quad in range(4):

@@ -25,7 +25,7 @@ SLOT_BLOCKS = [slice(0, 64), slice(64, 192), slice(192, 352), slice(352, 512)]
 VECTOR_BLOCK = 1
 EARLY_ROWS = 88
 QUERY_HALVES = [slice(0, P), slice(P, NQ)]
-QUERY_PIECES = [slice(q, q + 64) for q in range(0, NQ, 64)]
+QUERY_PIECES = [slice(0, 128), slice(128, 192), slice(192, 256)]
 
 
 def tile_attend_plw_rope_f_topk_kernel(tc, qT, kT, cT, wT, ls, offs, offs2, out_0, out_1, out_2):
@@ -151,8 +151,7 @@ def tile_attend_plw_rope_f_topk_kernel(tc, qT, kT, cT, wT, ls, offs, offs2, out_
 
         u_codes = [sb.tile([P, P], U32, name="u_codes%d" % r, align_bytes=64) for r in range(4)]
         u_scales = [sb.tile([P, P], U8, name="u_scales%d" % r, align_bytes=64) for r in range(4)]
-        early = [ps.tile([P, NQ], F32, name="early%d" % r) for r in range(2)]
-        late = [ps.tile([P, 2, P], F32, name="late%d" % h) for h in range(2)]
+        banks = [[ps.tile([P, P], F32, name="scores%d%d" % (r, h), tag="bank%d" % (2 * r + h)) for h in range(2)] for r in range(4)]
 
         def quantize_queries(qs):
             nc.vector.quantize_mx(out=q_codes[:, qs].bitcast(FP8X4), scales=q_scales[:, qs], in_=q_bf[:, 4 * qs.start : 4 * qs.stop])
@@ -160,39 +159,31 @@ def tile_attend_plw_rope_f_topk_kernel(tc, qT, kT, cT, wT, ls, offs, offs2, out_
         def quantize_keys(r):
             nc.vector.quantize_mx(out=u_codes[r][:].bitcast(FP8X4), scales=u_scales[r][:], in_=u_bf[r][:])
 
-        def scores(out, r, qs):
+        def scores(r, h):
+            qs = QUERY_HALVES[h]
             nc.tensor.matmul_mx(
-                out=out, lhsT=u_codes[r][:].bitcast(FP8X4), lhsT_scale=u_scales[r][:],
+                out=banks[r][h][:], lhsT=u_codes[r][:].bitcast(FP8X4), lhsT_scale=u_scales[r][:],
                 rhs=q_codes[:, qs].bitcast(FP8X4), rhs_scale=q_scales[:, qs], start=True, stop=True,
             )
 
+        passes = [(0, 0), (0, 1), (1, 0), (1, 1), (2, 0), (3, 0), (2, 1), (3, 1)]
         quantize_queries(QUERY_HALVES[0])
         quantize_keys(0)
-        scores(early[0][:, QUERY_HALVES[0]], 0, QUERY_HALVES[0])
         quantize_queries(QUERY_HALVES[1])
-        scores(early[0][:, QUERY_HALVES[1]], 0, QUERY_HALVES[1])
-        quantize_keys(1)
-        scores(early[1][:], 1, slice(0, NQ))
-        quantize_keys(2)
-        quantize_keys(3)
-        for h, qs in enumerate(QUERY_HALVES):
-            for r in (2, 3):
-                scores(late[h][:, r - 2, :], r, qs)
+        for r in range(1, 4):
+            quantize_keys(r)
+        for r, h in passes:
+            scores(r, h)
 
         y = sb.tile([P, 4, NQ], F32, name="y")
+        shifted = shared.tile([P, 4, NQ], F32, name="shifted", offset=3 * P * 4 * 2, align_bytes=64)
         out_rows = out_0.rearrange("(p r) q -> p r q", r=4)
-        for r in range(2):
-            shifted = shared.tile([P, NQ], F32, name="shifted%d" % r, offset=2560 + 1024 * r, align_bytes=64)
-            nc.vector.tensor_tensor(shifted[:], early[r][:], ls_wide[:], SUB)
-            nc.scalar.activation(y[:, r, :], shifted[:], EXP)
-        nc.sync.dma_start(out_rows[:, 0:2, :], y[:, 0:2, :])
-        for qs in QUERY_PIECES:
-            width = qs.stop - qs.start
-            shifted = sb.tile([P, 2, width], F32, name="shifted_late%d" % qs.start)
-            bank = late[qs.start // P][:, :, qs.start % P : qs.start % P + width]
-            nc.vector.tensor_tensor(shifted[:], bank, ls_wide[:, qs].unsqueeze(1).to_broadcast([P, 2, width]), SUB)
-            nc.scalar.activation(y[:, 2:4, qs], shifted[:], EXP)
-        nc.sync.dma_start(out_rows[:, 2:4, :], y[:, 2:4, :])
+        for r, h in passes:
+            for qs in QUERY_PIECES[1:] if (r, h) == passes[-1] else [QUERY_HALVES[h]]:
+                nc.vector.tensor_tensor(shifted[:, r, qs], banks[r][h][:, qs.start - h * P : qs.stop - h * P], ls_wide[:, qs], SUB)
+                nc.scalar.activation(y[:, r, qs], shifted[:, r, qs], EXP)
+            if h == 1 and r % 2 == 1:
+                nc.sync.dma_start(out_rows[:, r - 1 : r + 1, :], y[:, r - 1 : r + 1, :])
 
         y_bf = sb.tile([P, 4 * NQ], BF16, name="y_bf", align_bytes=64)
         y_codes = sb.tile([P, NQ], U32, name="y_codes", align_bytes=64)

@@ -23,9 +23,10 @@ P = 128
 
 SLOT_BLOCKS = [slice(0, 64), slice(64, 192), slice(192, 352), slice(352, 512)]
 VECTOR_BLOCK = 1
-EARLY_ROWS = 88
+FUSED = 128
+LAST_BLOCKS = [slice(128, 256), slice(256, 384), slice(384, 512)]
 QUERY_HALVES = [slice(0, P), slice(P, NQ)]
-QUERY_PIECES = [slice(0, 128), slice(128, 192), slice(192, 256)]
+QUERY_PIECES = [slice(q, q + 64) for q in range(0, NQ, 64)]
 
 
 def tile_attend_plw_rope_f_topk_kernel(tc, qT, kT, cT, wT, ls, offs, offs2, out_0, out_1, out_2):
@@ -86,24 +87,24 @@ def tile_attend_plw_rope_f_topk_kernel(tc, qT, kT, cT, wT, ls, offs, offs2, out_
                 elif row == 0:
                     nc.vector.tensor_scalar_mul(trig[j][:, 2, :], trig[j][:, 0, :], -1.0)
 
-        words = [sb.tile([P, 2, P], F32, name="words%d" % r) for r in range(4)]
+        words = sb.tile([P, 4, 2, P], F32, name="words")
 
         vector_block_tags = ("kg01", "kg03", "prod0", "kg23")
 
-        def products(t):
+        def products(t, blocks=SLOT_BLOCKS, vector_block=VECTOR_BLOCK):
             rows = slice(0, 2) if t % 2 == 0 else slice(1, 3)
             prod = sb.tile([P, 4, P, 2], F32, name="prod%d" % t, tag="prod%d" % t)
             keys = []
-            for b, slots in enumerate(SLOT_BLOCKS):
-                tag = vector_block_tags[t] if b == VECTOR_BLOCK else "kg%d%d" % (t, b)
+            for b, slots in enumerate(blocks):
+                tag = vector_block_tags[t] if b == vector_block else "kg%d%d" % (t, b)
                 kg = sb.tile([P, slots.stop - slots.start], F32, name="kg%d%d" % (t, b), tag=tag)
                 listed = k_win[t][:].indirect(tok[:, slots.start // 16 : slots.stop // 16])
-                if b == VECTOR_BLOCK:
+                if b == vector_block:
                     nc.vector.tensor_copy(kg[:], listed)
                 else:
                     nc.scalar.activation(kg[:], listed, COPY)
                 keys.append(kg)
-            for kg, slots in zip(keys, SLOT_BLOCKS):
+            for kg, slots in zip(keys, blocks):
                 s_rows = slice(slots.start // 4, slots.stop // 4)
                 nc.vector.tensor_tensor(
                     prod[:, :, s_rows, :].rearrange("p r s e -> p s r e"),
@@ -115,7 +116,7 @@ def tile_attend_plw_rope_f_topk_kernel(tc, qT, kT, cT, wT, ls, offs, offs2, out_
 
         def pair_sum(j, even, odd, r, s_rows):
             nc.vector.tensor_tensor(
-                words[r][:, j, s_rows].bitcast(BF16),
+                words[:, r, j, s_rows].bitcast(BF16),
                 even[:, r, s_rows, :].rearrange("p s e -> p (s e)"),
                 odd[:, r, s_rows, :].rearrange("p s e -> p (s e)"),
                 SUB,
@@ -126,24 +127,33 @@ def tile_attend_plw_rope_f_topk_kernel(tc, qT, kT, cT, wT, ls, offs, offs2, out_
         for r in range(4):
             pair_sum(0, first[0], first[1], r, slice(0, P))
         factors(1)
-        second = [products(2), products(3)]
+        even = products(2)
+        fused = sb.tile([P, 2, FUSED], F32, name="fused", tag="kg23")
+        for e in range(2):
+            nc.vector.tensor_tensor(fused[:, e, :], k_win[3][:].indirect(tok[:, 0 : FUSED // 16]), trig[1][:, 1 + e, 0:FUSED], MULT)
+        second = [even, products(3, LAST_BLOCKS, None)]
 
         q_bf = sb.tile([P, NQ * 4], BF16, name="q_bf", align_bytes=64)
         q_codes = sb.tile([P, NQ], U32, name="q_codes", align_bytes=64)
         q_scales = sb.tile([P, NQ], U8, name="q_scales", align_bytes=64)
         nc.scalar.copy(q_bf[:].rearrange("p (c i t) -> p c t i", i=4, t=4), q_raw[:].rearrange("p t (c i) -> p c t i", i=4))
 
-        pair_sum(1, second[0], second[1], 0, slice(0, EARLY_ROWS))
-        pair_sum(1, second[0], second[1], 0, slice(EARLY_ROWS, P))
-        for r in range(1, 4):
-            pair_sum(1, second[0], second[1], r, slice(0, P))
+        rows = FUSED // 4
+        nc.vector.tensor_tensor(
+            words[:, :, 1, 0:rows].bitcast(BF16).rearrange("p r (s e) -> p s r e", e=2),
+            even[:, :, 0:rows, :].rearrange("p r s e -> p s r e"),
+            fused[:].rearrange("p e (s r) -> p s r e", r=4),
+            SUB,
+        )
+        for r in range(4):
+            pair_sum(1, second[0], second[1], r, slice(rows, P))
 
         u_bf = [shared.tile([P, P * 4], BF16, name="u_bf%d" % r, offset=r * P * 4 * 2, align_bytes=64) for r in range(4)]
 
         def interleave(copy, r):
             copy(
                 u_bf[r][:].bitcast(F32).rearrange("p (c i j) -> p c j i", i=2, j=2),
-                words[r][:].rearrange("p j (c i) -> p c j i", i=2),
+                words[:, r].rearrange("p j (c i) -> p c j i", i=2),
             )
 
         for r in range(4):
@@ -179,7 +189,7 @@ def tile_attend_plw_rope_f_topk_kernel(tc, qT, kT, cT, wT, ls, offs, offs2, out_
         shifted = shared.tile([P, 4, NQ], F32, name="shifted", offset=3 * P * 4 * 2, align_bytes=64)
         out_rows = out_0.rearrange("(p r) q -> p r q", r=4)
         for r, h in passes:
-            for qs in QUERY_PIECES[1:] if (r, h) == passes[-1] else [QUERY_HALVES[h]]:
+            for qs in QUERY_PIECES[2:] if (r, h) == passes[-1] else [QUERY_HALVES[h]]:
                 nc.vector.tensor_tensor(shifted[:, r, qs], banks[r][h][:, qs.start - h * P : qs.stop - h * P], ls_wide[:, qs], SUB)
                 nc.scalar.activation(y[:, r, qs], shifted[:, r, qs], EXP)
             if h == 1 and r % 2 == 1:
@@ -195,9 +205,14 @@ def tile_attend_plw_rope_f_topk_kernel(tc, qT, kT, cT, wT, ls, offs, offs2, out_
                 y[:, quarters, qs].rearrange("p r (c i) -> p c r i", i=4),
             )
 
-        for qs in QUERY_HALVES:
-            round_result(slice(0, 2), qs)
-        for qs in QUERY_PIECES:
+        last = QUERY_PIECES[-1]
+        nc.scalar.activation(
+            y_bf[:, 4 * last.start : 4 * last.stop].rearrange("p (c i r) -> p c r i", i=4, r=4),
+            shifted[:, :, last].rearrange("p r (c i) -> p c r i", i=4),
+            EXP,
+        )
+        round_result(slice(0, 2), slice(0, last.start))
+        for qs in QUERY_PIECES[:-1]:
             round_result(slice(2, 4), qs)
         for qs in QUERY_PIECES:
             nc.vector.quantize_mx(out=y_codes[:, qs].bitcast(FP8X4), scales=y_scales[:, qs], in_=y_bf[:, 4 * qs.start : 4 * qs.stop])

@@ -23,6 +23,8 @@ P = 128
 
 SLOT_BLOCKS = [slice(0, 64), slice(64, 192), slice(192, 352), slice(352, 512)]
 VECTOR_BLOCK = 1
+OWN = 192
+EVEN_BLOCKS = [slice(0, 64), slice(64, 256), slice(256, 384), slice(384, 512)]
 FUSED = 128
 LAST_BLOCKS = [slice(128, 256), slice(256, 384), slice(384, 512)]
 QUERY_HALVES = [slice(0, P), slice(P, NQ)]
@@ -74,18 +76,21 @@ def tile_attend_plw_rope_f_topk_kernel(tc, qT, kT, cT, wT, ls, offs, offs2, out_
         ls_wide = sb.tile([P, NQ], F32, name="ls_wide")
         nc.scalar.copy(ls_wide[:], ls_wide_ps[:].rearrange("p h q -> p (h q)"))
 
-        trig = [sb.tile([P, 3, N], F32, name="trig%d" % j) for j in range(2)]
+        trig = [sb.tile([P, 3, width], F32, name="trig%d" % j) for j, width in enumerate((N, 3 * N - OWN))]
 
         def factors(j):
             for row, win in ((0, c_win[j]), (1, w_win[j])):
                 if j == 0:
                     nc.vector.tensor_copy(trig[j][:, row, :], win[:].indirect(pos[:]))
+                elif row == 0:
+                    nc.scalar.activation(trig[j][:, row, 0:N], win[:].indirect(pos[:]), COPY)
                 else:
-                    nc.scalar.activation(trig[j][:, row, :], win[:].indirect(pos[:]), COPY)
+                    nc.scalar.activation(trig[j][:, row, OWN:N], win[:].indirect(pos[:, OWN // 16 :]), COPY)
+                    nc.vector.tensor_copy(trig[j][:, row, 0:OWN], win[:].indirect(pos[:, 0 : OWN // 16]))
                 if row == 0 and j == 0:
                     nc.scalar.mul(trig[j][:, 2, :], trig[j][:, 0, :], -1.0)
                 elif row == 0:
-                    nc.vector.tensor_scalar_mul(trig[j][:, 2, :], trig[j][:, 0, :], -1.0)
+                    nc.vector.tensor_scalar_mul(trig[j][:, 2, 0:N], trig[j][:, 0, 0:N], -1.0)
 
         words = sb.tile([P, 4, 2, P], F32, name="words")
 
@@ -93,7 +98,10 @@ def tile_attend_plw_rope_f_topk_kernel(tc, qT, kT, cT, wT, ls, offs, offs2, out_
 
         def products(t, blocks=SLOT_BLOCKS, vector_block=VECTOR_BLOCK):
             rows = slice(0, 2) if t % 2 == 0 else slice(1, 3)
-            prod = sb.tile([P, 4, P, 2], F32, name="prod%d" % t, tag="prod%d" % t)
+            if t == 1:
+                prod = trig[1][:].rearrange("p e n -> p (e n)")[:, N : 3 * N].rearrange("p (r s e) -> p r s e", r=4, e=2)
+            else:
+                prod = sb.tile([P, 4, P, 2], F32, name="prod%d" % t, tag="prod%d" % t)
             keys = []
             for b, slots in enumerate(blocks):
                 tag = vector_block_tags[t] if b == vector_block else "kg%d%d" % (t, b)
@@ -127,7 +135,7 @@ def tile_attend_plw_rope_f_topk_kernel(tc, qT, kT, cT, wT, ls, offs, offs2, out_
         for r in range(4):
             pair_sum(0, first[0], first[1], r, slice(0, P))
         factors(1)
-        even = products(2)
+        even = products(2, EVEN_BLOCKS)
         fused = sb.tile([P, 2, FUSED], F32, name="fused", tag="kg23")
         for e in range(2):
             nc.vector.tensor_tensor(fused[:, e, :], k_win[3][:].indirect(tok[:, 0 : FUSED // 16]), trig[1][:, 1 + e, 0:FUSED], MULT)

from contextlib import ExitStack

import concourse.mybir as mybir
from concourse.masks import make_identity

N, T, D, NQ, NPOS = 512, 2048, 512, 256, 1024
FLOPS = 2 * N * D * NQ
BYTES = 4 * (D * NQ + D * T + D * NPOS + NQ + N * NQ) + 2 * 128 * 32 * 2 + 128 * NQ * 4 + 16 * NQ

F32 = mybir.dt.float32
BF16 = mybir.dt.bfloat16
I32 = mybir.dt.int32
U32 = mybir.dt.uint32
U16 = mybir.dt.uint16
U8 = mybir.dt.uint8
FP8X4 = mybir.dt.float8_e4m3fn_x4
MULT = mybir.AluOpType.mult
SUB = mybir.AluOpType.subtract
EXP = mybir.ActivationFunctionType.Exp
COPY = mybir.ActivationFunctionType.Copy

P = 128

SLOT_BLOCKS = [slice(0, 64), slice(64, 192), slice(192, 352), slice(352, 512)]
VECTOR_BLOCK = 1
OWN = 192
EVEN_BLOCKS = [slice(0, 64), slice(64, 256), slice(256, 384), slice(384, 512)]
FUSED = 128
LAST_BLOCKS = [slice(128, 256), slice(256, 384), slice(384, 512)]
QUERY_HALVES = [slice(0, P), slice(P, NQ)]
QUERY_PIECES = [slice(q, q + 64) for q in range(0, NQ, 64)]


def tile_attend_plw_rope_f_topk_kernel(tc, qT, kT, cT, wT, ls, offs, offs2, out_0, out_1, out_2):
    nc = tc.nc
    with ExitStack() as ctx:
        sb = ctx.enter_context(tc.tile_pool(name="sb", bufs=1))
        shared = ctx.enter_context(tc.tile_pool(name="shared", bufs=1))
        ps = ctx.enter_context(tc.psum_pool(name="ps", bufs=1))

        tok = sb.tile([P, N // 16], U16, name="tok")
        pos = sb.tile([P, N // 16], U16, name="pos")
        k_rows = kT.rearrange("(p t) n -> p t n", t=4)
        c_rows = cT.rearrange("(p t) n -> p t n", t=4)
        w_rows = wT.rearrange("(p t) n -> p t n", t=4)
        k_win = [sb.tile([P, T], F32, name="k_win%d" % t) for t in range(4)]
        c_win = [sb.tile([P, NPOS], F32, name="c_win%d" % j) for j in range(2)]
        w_win = [sb.tile([P, NPOS], F32, name="w_win%d" % j) for j in range(2)]
        q_raw = sb.tile([P, 4, NQ], F32, name="q_raw")
        ls_rows = sb.tile([P, P], F32, name="ls_rows")

        nc.gpsimd.memset(ls_rows[:], 0.0)
        nc.scalar.dma_start(ls_rows[0:2, :], ls[0, 0, :].rearrange("(h p) -> h p", p=P))
        nc.sync.dma_start(c_win[0][:], c_rows[:, 0, :])
        nc.sync.dma_start(pos[:], offs2)
        nc.sync.dma_start(w_win[0][:], w_rows[:, 0, :])
        nc.sync.dma_start(tok[:], offs)
        nc.sync.dma_start(k_win[0][:], k_rows[:, 0, :])
        nc.sync.dma_start(k_win[1][:], k_rows[:, 1, :])
        nc.sync.dma_start(c_win[1][:], c_rows[:, 2, :])
        nc.sync.dma_start(w_win[1][:], w_rows[:, 2, :])
        nc.sync.dma_start(k_win[2][:], k_rows[:, 2, :])
        nc.sync.dma_start(k_win[3][:], k_rows[:, 3, :])
        nc.sync.dma_start(q_raw[:], qT[0].rearrange("(p t) n -> p t n", t=4))

        ident = sb.tile([P, P], F32, name="ident")
        make_identity(nc, ident[:])

        ls_cols_ps = ps.tile([P, P], F32, name="ls_cols_ps", tag="bank7")
        nc.tensor.transpose(ls_cols_ps[:], ls_rows[:], ident[:])
        ls_cols = sb.tile([P, 2], F32, name="ls_cols")
        nc.scalar.copy(ls_cols[:], ls_cols_ps[:, 0:2])
        ls_wide_ps = ps.tile([P, 2, P], F32, name="ls_wide_ps", tag="bank6")
        for h in range(2):
            nc.tensor.transpose(ls_wide_ps[:, h, :], ls_cols[:, h : h + 1].to_broadcast([P, P]), ident[:])
        ls_wide = sb.tile([P, NQ], F32, name="ls_wide")
        nc.scalar.copy(ls_wide[:], ls_wide_ps[:].rearrange("p h q -> p (h q)"))

        trig = [sb.tile([P, 3, width], F32, name="trig%d" % j) for j, width in enumerate((N, 3 * N - OWN))]

        def factors(j):
            for row, win in ((0, c_win[j]), (1, w_win[j])):
                if j == 0:
                    nc.vector.tensor_copy(trig[j][:, row, :], win[:].indirect(pos[:]))
                elif row == 0:
                    nc.scalar.activation(trig[j][:, row, 0:N], win[:].indirect(pos[:]), COPY)
                else:
                    nc.scalar.activation(trig[j][:, row, OWN:N], win[:].indirect(pos[:, OWN // 16 :]), COPY)
                    nc.vector.tensor_copy(trig[j][:, row, 0:OWN], win[:].indirect(pos[:, 0 : OWN // 16]))
                if row == 0 and j == 0:
                    nc.scalar.mul(trig[j][:, 2, :], trig[j][:, 0, :], -1.0)
                elif row == 0:
                    nc.vector.tensor_scalar_mul(trig[j][:, 2, 0:N], trig[j][:, 0, 0:N], -1.0)

        words = sb.tile([P, 4, 2, P], F32, name="words")

        vector_block_tags = ("kg01", "kg03", "prod0", "kg23")

        def products(t, blocks=SLOT_BLOCKS, vector_block=VECTOR_BLOCK):
            rows = slice(0, 2) if t % 2 == 0 else slice(1, 3)
            if t == 1:
                prod = trig[1][:].rearrange("p e n -> p (e n)")[:, N : 3 * N].rearrange("p (r s e) -> p r s e", r=4, e=2)
            else:
                prod = sb.tile([P, 4, P, 2], F32, name="prod%d" % t, tag="prod%d" % t)
            keys = []
            for b, slots in enumerate(blocks):
                tag = vector_block_tags[t] if b == vector_block else "kg%d%d" % (t, b)
                kg = sb.tile([P, slots.stop - slots.start], F32, name="kg%d%d" % (t, b), tag=tag)
                listed = k_win[t][:].indirect(tok[:, slots.start // 16 : slots.stop // 16])
                if b == vector_block:
                    nc.vector.tensor_copy(kg[:], listed)
                else:
                    nc.scalar.activation(kg[:], listed, COPY)
                keys.append(kg)
            for kg, slots in zip(keys, blocks):
                s_rows = slice(slots.start // 4, slots.stop // 4)
                nc.vector.tensor_tensor(
                    prod[:, :, s_rows, :].rearrange("p r s e -> p s r e"),
                    kg[:].rearrange("p (s r) -> p s r", r=4).unsqueeze(3).to_broadcast([P, s_rows.stop - s_rows.start, 4, 2]),
                    trig[t // 2][:, rows, slots].rearrange("p e (s r) -> p s r e", r=4),
                    MULT,
                )
            return prod

        def pair_sum(j, even, odd, r, s_rows):
            nc.vector.tensor_tensor(
                words[:, r, j, s_rows].bitcast(BF16),
                even[:, r, s_rows, :].rearrange("p s e -> p (s e)"),
                odd[:, r, s_rows, :].rearrange("p s e -> p (s e)"),
                SUB,
            )

        factors(0)
        first = [products(0), products(1)]
        for r in range(4):
            pair_sum(0, first[0], first[1], r, slice(0, P))
        factors(1)
        even = products(2, EVEN_BLOCKS)
        fused = sb.tile([P, 2, FUSED], F32, name="fused", tag="kg23")
        for e in range(2):
            nc.vector.tensor_tensor(fused[:, e, :], k_win[3][:].indirect(tok[:, 0 : FUSED // 16]), trig[1][:, 1 + e, 0:FUSED], MULT)
        second = [even, products(3, LAST_BLOCKS, None)]

        q_bf = sb.tile([P, NQ * 4], BF16, name="q_bf", align_bytes=64)
        q_codes = sb.tile([P, NQ], U32, name="q_codes", align_bytes=64)
        q_scales = sb.tile([P, NQ], U8, name="q_scales", align_bytes=64)
        nc.scalar.copy(q_bf[:].rearrange("p (c i t) -> p c t i", i=4, t=4), q_raw[:].rearrange("p t (c i) -> p c t i", i=4))

        rows = FUSED // 4
        nc.vector.tensor_tensor(
            words[:, :, 1, 0:rows].bitcast(BF16).rearrange("p r (s e) -> p s r e", e=2),
            even[:, :, 0:rows, :].rearrange("p r s e -> p s r e"),
            fused[:].rearrange("p e (s r) -> p s r e", r=4),
            SUB,
        )
        for r in range(4):
            pair_sum(1, second[0], second[1], r, slice(rows, P))

        u_bf = [shared.tile([P, P * 4], BF16, name="u_bf%d" % r, offset=r * P * 4 * 2, align_bytes=64) for r in range(4)]

        def interleave(copy, r):
            copy(
                u_bf[r][:].bitcast(F32).rearrange("p (c i j) -> p c j i", i=2, j=2),
                words[:, r].rearrange("p j (c i) -> p c j i", i=2),
            )

        for r in range(4):
            interleave(nc.scalar.copy, r)

        u_codes = [sb.tile([P, P], U32, name="u_codes%d" % r, align_bytes=64) for r in range(4)]
        u_scales = [sb.tile([P, P], U8, name="u_scales%d" % r, align_bytes=64) for r in range(4)]
        banks = [[ps.tile([P, P], F32, name="scores%d%d" % (r, h), tag="bank%d" % (2 * r + h)) for h in range(2)] for r in range(4)]

        def quantize_queries(qs):
            nc.vector.quantize_mx(out=q_codes[:, qs].bitcast(FP8X4), scales=q_scales[:, qs], in_=q_bf[:, 4 * qs.start : 4 * qs.stop])

        def quantize_keys(r):
            nc.vector.quantize_mx(out=u_codes[r][:].bitcast(FP8X4), scales=u_scales[r][:], in_=u_bf[r][:])

        def scores(r, h):
            qs = QUERY_HALVES[h]
            nc.tensor.matmul_mx(
                out=banks[r][h][:], lhsT=u_codes[r][:].bitcast(FP8X4), lhsT_scale=u_scales[r][:],
                rhs=q_codes[:, qs].bitcast(FP8X4), rhs_scale=q_scales[:, qs], start=True, stop=True,
            )

        passes = [(0, 0), (0, 1), (1, 0), (1, 1), (2, 0), (3, 0), (2, 1), (3, 1)]
        quantize_queries(QUERY_HALVES[0])
        quantize_keys(0)
        quantize_queries(QUERY_HALVES[1])
        for r in range(1, 4):
            quantize_keys(r)
        for r, h in passes:
            scores(r, h)

        y = sb.tile([P, 4, NQ], F32, name="y")
        shifted = shared.tile([P, 4, NQ], F32, name="shifted", offset=3 * P * 4 * 2, align_bytes=64)
        out_rows = out_0.rearrange("(p r) q -> p r q", r=4)
        for r, h in passes:
            for qs in QUERY_PIECES[2:] if (r, h) == passes[-1] else [QUERY_HALVES[h]]:
                nc.vector.tensor_tensor(shifted[:, r, qs], banks[r][h][:, qs.start - h * P : qs.stop - h * P], ls_wide[:, qs], SUB)
                nc.scalar.activation(y[:, r, qs], shifted[:, r, qs], EXP)
            if h == 1 and r % 2 == 1:
                nc.sync.dma_start(out_rows[:, r - 1 : r + 1, :], y[:, r - 1 : r + 1, :])

        y_bf = sb.tile([P, 4 * NQ], BF16, name="y_bf", align_bytes=64)
        y_codes = sb.tile([P, NQ], U32, name="y_codes", align_bytes=64)
        y_scales = sb.tile([P, NQ], U8, name="y_scales", align_bytes=64)

        def round_result(quarters, qs):
            nc.vector.tensor_copy(
                y_bf[:, 4 * qs.start : 4 * qs.stop].rearrange("p (c i r) -> p c r i", i=4, r=4)[:, :, quarters],
                y[:, quarters, qs].rearrange("p r (c i) -> p c r i", i=4),
            )

        last = QUERY_PIECES[-1]
        nc.scalar.activation(
            y_bf[:, 4 * last.start : 4 * last.stop].rearrange("p (c i r) -> p c r i", i=4, r=4),
            shifted[:, :, last].rearrange("p r (c i) -> p c r i", i=4),
            EXP,
        )
        round_result(slice(0, 2), slice(0, last.start))
        for qs in QUERY_PIECES[:-1]:
            round_result(slice(2, 4), qs)
        for qs in QUERY_PIECES:
            nc.vector.quantize_mx(out=y_codes[:, qs].bitcast(FP8X4), scales=y_scales[:, qs], in_=y_bf[:, 4 * qs.start : 4 * qs.stop])

        nc.sync.dma_start(out_1[0].rearrange("p q x -> p (q x)").bitcast(I32), y_codes[:].bitcast(I32))
        for quad in range(4):
            queue = nc.scalar if quad % 2 == 0 else nc.sync
            queue.dma_start(out_2[0, 4 * quad : 4 * quad + 4, :].bitcast(I32), y_scales[32 * quad : 32 * quad + 4, :].bitcast(I32))
